import numpy as np
import ml_dtypes


def mxq(x, axis, fmt="e4m3"):
    dtype, down = {"e4m3": (ml_dtypes.float8_e4m3fn, 7), "e5m2": (ml_dtypes.float8_e5m2, 14)}[fmt]
    v = np.moveaxis(np.asarray(x, np.float32).astype(ml_dtypes.bfloat16).astype(np.float64), axis, -1)
    blocks = v.reshape(v.shape[:-1] + (-1, 32))
    amax = np.abs(blocks).max(-1, keepdims=True)
    byte = np.maximum(np.where(amax > 0, np.frexp(amax)[1] - 1 + 127, 0) - down, 1)
    scale = np.exp2(byte - 127.0)
    codes = (blocks / scale).astype(np.float32).astype(dtype).astype(np.float64)
    return np.moveaxis((codes * scale).reshape(v.shape), -1, axis)


WIDE = False


def mx_kscale(k):
    if not WIDE:
        return np.ones(k)
    levels = np.array([10, -10, 5, -5, 0])
    if k % 512:
        return np.exp2(np.random.permutation(np.resize(levels, k // 32))).repeat(32)
    a = np.empty((k // 512, 16))
    for p in range(k // 512):
        a[p, :8] = np.random.permutation(np.resize(levels, 8))
        for g in range(8):
            far = levels[np.abs(levels - a[p, g]) >= 10]
            a[p, g + 8] = far[np.random.randint(len(far))]
    return np.exp2(a.ravel()).repeat(32)


def f64(x):
    return np.asarray(x).astype(np.float64)


def striped(idx):
    return np.tile(idx.reshape(-1, 16).T, (8, 1)).astype(np.uint16)


def unstriped(offs):
    return offs[:16].T.reshape(-1).astype(np.int64)


def relu(v):
    return np.maximum(v, 0.0)


K, T, E, C, H, N = 512, 512, 8, 128, 1024, 128


def by_expert(wq, xq):
    return np.concatenate([wq[e].T @ xq[:, e * C:(e + 1) * C] for e in range(E)], axis=1)


def setup_inputs():
    n = np.random.standard_normal
    s = mx_kscale(K)[:, None]
    u = mx_kscale(H)
    first = np.random.permutation(np.repeat(np.arange(E), T // E))
    second = (first + 1 + np.random.permutation(np.repeat(np.arange(E - 1), -(-T // (E - 1)))[:T])) % E
    while np.bincount(second, minlength=E).max() != T // E:
        load = np.bincount(second, minlength=E); hi, lo = int(load.argmax()), int(load.argmin())
        t = np.flatnonzero((second == hi) & (first != lo))[0]; second[t] = lo
    slot_token = np.empty(E * C, np.int64); pos = np.empty((2, T), np.int64); fill = np.zeros(E, np.int64)
    place = np.stack([np.random.permutation(C) for _ in range(E)])
    for r, deal in enumerate((first, second)):
        for t in np.random.permutation(T):
            e = deal[t]; j = e * C + place[e, fill[e]]; fill[e] += 1; slot_token[j] = t; pos[r, t] = j
    g = np.random.uniform(0.2, 0.8, T)
    return {
        "xT": (n((K, T)) * s).astype(np.float32),
        "w1": (n((E, K, H)) / np.sqrt(K) / s[None] * u[None, None, :]).astype(np.float32),
        "w2": (n((E, H, N)) / np.sqrt(H) / u[None, :, None]).astype(np.float32),
        "gate": np.stack([np.tile(g, (N, 1)), np.tile(1.0 - g, (N, 1))]).astype(np.float32),
        "offs": striped(slot_token),
        "pos1": striped(pos[0]),
        "pos2": striped(pos[1]),
    }


def reference(xT, w1, w2, gate, offs, pos1, pos2):
    idx = unstriped(offs)
    xq = mxq(f64(xT)[:, idx], 0, "e4m3")
    h = relu(by_expert(mxq(f64(w1), 1, "e4m3"), xq))
    y = by_expert(mxq(f64(w2), 1, "e4m3"), mxq(h, 0, "e4m3"))
    return f64(gate[0]) * y[:, unstriped(pos1)] + f64(gate[1]) * y[:, unstriped(pos2)]

@@ -1,0 +1,186 @@
+from contextlib import ExitStack
+
+import concourse.mybir as mybir
+
+F32 = mybir.dt.float32
+BF16 = mybir.dt.bfloat16
+U32 = mybir.dt.uint32
+U16 = mybir.dt.uint16
+U8 = mybir.dt.uint8
+FP8X4 = mybir.dt.float8_e4m3fn_x4
+RELU = mybir.ActivationFunctionType.Relu
+MULT = mybir.AluOpType.mult
+MAX = mybir.AluOpType.max
+
+P = 128
+K, T, E, C, H, N = 512, 512, 8, 128, 1024, 128
+S = E * C
+HALF = 512
+W2_LOADS = ((0, 2, 4), (2, 4, 4), (4, 5, 0), (5, 7, 4), (7, 8, 0))
+FLOPS = 2 * S * K * H + 2 * S * H * N
+
+
+def tile_routed_moe_kernel(tc, xT, w1, w2, gate, offs, pos1, pos2, out):
+    nc = tc.nc
+    with ExitStack() as ctx:
+        keep = ctx.enter_context(tc.tile_pool(name="keep", bufs=1))
+        raw = ctx.enter_context(tc.tile_pool(name="raw", bufs=8))
+        work = ctx.enter_context(tc.tile_pool(name="work", bufs=3))
+        hold = ctx.enter_context(tc.tile_pool(name="hold", bufs=4))
+        ps_a = ctx.enter_context(tc.psum_pool(name="ps_a", bufs=5))
+        ps_y = ctx.enter_context(tc.psum_pool(name="ps_y", bufs=2))
+
+        offs_t = keep.tile([P, S // 16], U16)
+        pos1_t = keep.tile([P, T // 16], U16)
+        pos2_t = keep.tile([P, T // 16], U16)
+        x_raw = keep.tile([P, 4, T], F32)
+        nc.sync.dma_start(out=x_raw[:], in_=xT.rearrange("(p j) t -> p j t", j=4))
+        nc.sync.dma_start(offs_t[:], offs)
+        nc.sync.dma_start(pos1_t[:], pos1)
+        nc.sync.dma_start(pos2_t[:], pos2)
+        w1_raw = {}
+        for e in range(E):
+            parts = 2 if e == 0 else 1
+            width = H // parts
+            for i in range(parts):
+                tile = raw.tile([P, 4, width], F32, name="raw")
+                src = w1[e, :, i * width:(i + 1) * width].rearrange("(p j) c -> p j c", j=4)
+                nc.sync.dma_start(out=tile[:], in_=src)
+                for q in range(2 // parts):
+                    w1_raw[e, i + q] = tile[:, :, q * HALF:(q + 1) * HALF]
+        w2_raw = {}
+        for a, b, split in W2_LOADS:
+            w2_raw[a] = raw.tile([P, 2 * (b - a), 4, N], F32, name="raw")
+            src = w2[a:b, :, :].rearrange("e (q p j) n -> p (e q) (j n)", p=P, j=4)
+            nc.sync.dma_start(out=w2_raw[a][:].rearrange("p q j n -> p q (j n)"), in_=src)
+        gate_t = raw.tile([P, 2, T], F32, name="raw")
+        nc.sync.dma_start(out=gate_t[:], in_=gate.rearrange("r p t -> p r t"))
+
+        x_bf = keep.tile([P, T, 4], BF16, align_bytes=64)
+        x_words = keep.tile([P, T], U32, align_bytes=64)
+        x_bytes = keep.tile([P, T], U8, align_bytes=64)
+        nc.gpsimd.memset(x_bytes[:], 0)
+        x_src = x_raw[:].rearrange("p j (c i) -> p c j i", i=4)
+        x_dst = x_bf[:].rearrange("p (c i) j -> p c j i", i=4)
+        nc.vector.tensor_copy(out=x_dst[:, 0:64], in_=x_src[:, 0:64])
+        nc.scalar.copy(out=x_dst[:, 64:128], in_=x_src[:, 64:128])
+        nc.vector.quantize_mx(out=x_words[:].bitcast(FP8X4), scales=x_bytes[:], in_=x_bf[:].rearrange("p t j -> p (t j)"))
+        g_words = keep.tile([P, S], U32, align_bytes=64)
+        g_bytes = keep.tile([P, S], U8, align_bytes=64)
+
+        def gather(a, b):
+            lst = offs_t[:, a // 16:b // 16]
+            nc.vector.tensor_copy(g_words[:, a:b], x_words[:].indirect(lst))
+            nc.vector.tensor_copy(g_bytes[:, a:b], x_bytes[:].indirect(lst))
+
+        gathers = {0: (0, 256), 1: (256, 640), 2: (640, 1024)}
+
+        y_all = keep.tile([P, S], F32)
+
+        def cast_w1(e, q):
+            grouped = work.tile([P, 4, P, 4], BF16, name="w1_bf", align_bytes=64)
+            src = w1_raw[e, q].rearrange("p j (m u v) -> p u m j v", u=2, v=2)
+            dst = grouped[:].rearrange("p (u v) m j -> p u m j v", u=2)
+            if q == 0 or e == 0:
+                nc.scalar.copy(out=dst, in_=src)
+            else:
+                nc.vector.tensor_copy(out=dst, in_=src)
+            return grouped
+
+        def quant_w1(grouped):
+            words = work.tile([P, HALF], U32, name="w1_words", align_bytes=64, bufs=4)
+            scales = work.tile([P, HALF], U8, name="w1_scales", align_bytes=64, bufs=4)
+            nc.vector.quantize_mx(out=words[:].bitcast(FP8X4), scales=scales[:], in_=grouped[:].rearrange("p t m j -> p (t m j)"))
+            return words, scales
+
+        def cast_w2(a, b, split):
+            grouped = work.tile([P, 2 * (b - a), N, 4], BF16, name="w2_bf", align_bytes=64, bufs=2)
+            src = w2_raw[a][:].rearrange("p q j (c i) -> p q c j i", i=4)
+            dst = grouped[:].rearrange("p q (c i) j -> p q c j i", i=4)
+            if split > 0:
+                nc.vector.tensor_copy(out=dst[:, 0:split], in_=src[:, 0:split])
+            if split < 2 * (b - a):
+                nc.scalar.copy(out=dst[:, split:], in_=src[:, split:])
+            return grouped
+
+        def quant_w2(grouped, n):
+            words = work.tile([P, n * N], U32, name="w2_words", align_bytes=64, bufs=2)
+            scales = work.tile([P, n * N], U8, name="w2_scales", align_bytes=64, bufs=2)
+            nc.vector.quantize_mx(out=words[:].bitcast(FP8X4), scales=scales[:], in_=grouped[:].rearrange("p q n j -> p (q n j)"))
+            return words, scales
+
+        def layer1(e, w):
+            words, scales = w
+            bank = ps_a.tile([P, 4 * C], F32, name="h_bank")
+            slots = slice(e * C, (e + 1) * C)
+            for t in range(4):
+                cols = slice(t * P, (t + 1) * P)
+                nc.tensor.matmul_mx(
+                    out=bank[:, t * C:(t + 1) * C],
+                    lhsT=words[:, cols].bitcast(FP8X4), lhsT_scale=scales[:, cols],
+                    rhs=g_words[:, slots].bitcast(FP8X4), rhs_scale=g_bytes[:, slots],
+                    start=True, stop=True,
+                )
+            return bank
+
+        def relu(e, banks, h, zero):
+            for q in range(2):
+                src = banks[q][:].rearrange("p (t n) -> p n t", t=4)
+                if q == 1 and e in (1, 3, 5):
+                    nc.vector.tensor_scalar(out=h[:, e % 2, q], in0=src, scalar1=zero, scalar2=None, op0=MAX)
+                else:
+                    nc.scalar.activation(out=h[:, e % 2, q], in_=src, func=RELU, bias=zero)
+
+        def quant_h(h):
+            words = hold.tile([P, 4 * C], U32, name="h_words", align_bytes=64)
+            scales = hold.tile([P, 4 * C], U8, name="h_scales", align_bytes=64)
+            nc.vector.quantize_mx(out=words[:].bitcast(FP8X4), scales=scales[:], in_=h[:].rearrange("p e q n t -> p (e q n t)"))
+            return words, scales
+
+        def layer2(e, w, first, hq):
+            bank = ps_y.tile([P, C], F32, name="y_bank")
+            for q in range(2):
+                cols = slice((first + q) * N, (first + q + 1) * N)
+                slots = slice((2 * (e % 2) + q) * C, (2 * (e % 2) + q + 1) * C)
+                nc.tensor.matmul_mx(
+                    out=bank[:],
+                    lhsT=w[0][:, cols].bitcast(FP8X4), lhsT_scale=w[1][:, cols],
+                    rhs=hq[0][:, slots].bitcast(FP8X4), rhs_scale=hq[1][:, slots],
+                    start=(q == 0), stop=(q == 1),
+                )
+            nc.scalar.copy(out=y_all[:, e * C:(e + 1) * C], in_=bank[:])
+
+        h_codes = []
+        banks = {}
+        h = None
+        for e in range(E):
+            if e in gathers:
+                gather(*gathers[e])
+            halves = [cast_w1(e, q) for q in range(2)]
+            if e > 0:
+                zero = work.tile([P, 1], F32, name="zero")
+                nc.gpsimd.tensor_scalar(out=zero[:], in0=halves[1][:, 3, P - 1, 3:4], scalar1=0.0, scalar2=None, op0=MULT)
+                if e % 2 == 1:
+                    h = work.tile([P, 2, 2, C, 4], BF16, name="h_bf", align_bytes=64, bufs=2)
+                relu(e - 1, banks, h, zero[:])
+                if e % 2 == 0:
+                    h_codes.append(quant_h(h))
+            banks = {}
+            for q in (1, 0):
+                banks[q] = layer1(e, quant_w1(halves[q]))
+        relu(E - 1, banks, h, 0.0)
+        for a, b, split in W2_LOADS:
+            g = cast_w2(a, b, split)
+            if a == 0:
+                h_codes.append(quant_h(h))
+            w = quant_w2(g, 2 * (b - a))
+            for e in range(a, b):
+                layer2(e, w, 2 * (e - a), h_codes[e // 2])
+
+        part1 = keep.tile([P, T], F32)
+        part2 = keep.tile([P, T], F32)
+        result = keep.tile([P, T], F32)
+        nc.vector.tensor_tensor(part1[:], y_all[:].indirect(pos1_t[:]), gate_t[:, 0, :], MULT)
+        nc.vector.tensor_tensor(part2[:], y_all[:].indirect(pos2_t[:]), gate_t[:, 1, :], MULT)
+        nc.vector.tensor_add(result[:], part1[:], part2[:])
+        nc.sync.dma_start(out=out, in_=result[:])

@@ -10,13 +10,17 @@ U8 = mybir.dt.uint8
 FP8X4 = mybir.dt.float8_e4m3fn_x4
 RELU = mybir.ActivationFunctionType.Relu
 MULT = mybir.AluOpType.mult
-MAX = mybir.AluOpType.max
 
 P = 128
 K, T, E, C, H, N = 512, 512, 8, 128, 1024, 128
 S = E * C
 HALF = 512
-W2_LOADS = ((0, 2, 4), (2, 4, 4), (4, 5, 0), (5, 7, 4), (7, 8, 0))
+W2_LOADS = ((0, 2, 2), (2, 4, 2), (4, 6, 2), (6, 7, 0), (7, 8, 1))
+Y_BANKS = ((0, 4), (4, 7), (7, 8))
+SHARED = (6,)
+TIED = 6
+Y_AFTER = 7
+H_LAST_IN = 0
 FLOPS = 2 * S * K * H + 2 * S * H * N
 
 
@@ -26,9 +30,8 @@ def tile_routed_moe_kernel(tc, xT, w1, w2, gate, offs, pos1, pos2, out):
         keep = ctx.enter_context(tc.tile_pool(name="keep", bufs=1))
         raw = ctx.enter_context(tc.tile_pool(name="raw", bufs=8))
         work = ctx.enter_context(tc.tile_pool(name="work", bufs=3))
-        hold = ctx.enter_context(tc.tile_pool(name="hold", bufs=4))
         ps_a = ctx.enter_context(tc.psum_pool(name="ps_a", bufs=5))
-        ps_y = ctx.enter_context(tc.psum_pool(name="ps_y", bufs=2))
+        ps_y = ctx.enter_context(tc.psum_pool(name="ps_y", bufs=3))
 
         offs_t = keep.tile([P, S // 16], U16)
         pos1_t = keep.tile([P, T // 16], U16)
@@ -36,24 +39,22 @@ def tile_routed_moe_kernel(tc, xT, w1, w2, gate, offs, pos1, pos2, out):
         x_raw = keep.tile([P, 4, T], F32)
         nc.sync.dma_start(out=x_raw[:], in_=xT.rearrange("(p j) t -> p j t", j=4))
         nc.sync.dma_start(offs_t[:], offs)
-        nc.sync.dma_start(pos1_t[:], pos1)
-        nc.sync.dma_start(pos2_t[:], pos2)
-        w1_raw = {}
+        w1_raw = []
         for e in range(E):
-            parts = 2 if e == 0 else 1
-            width = H // parts
-            for i in range(parts):
-                tile = raw.tile([P, 4, width], F32, name="raw")
-                src = w1[e, :, i * width:(i + 1) * width].rearrange("(p j) c -> p j c", j=4)
-                nc.sync.dma_start(out=tile[:], in_=src)
-                for q in range(2 // parts):
-                    w1_raw[e, i + q] = tile[:, :, q * HALF:(q + 1) * HALF]
+            tile = raw.tile([P, 4, H], F32, name="raw", align_bytes=64)
+            nc.sync.dma_start(out=tile[:], in_=w1[e].rearrange("(p j) c -> p j c", j=4))
+            w1_raw.append(tile)
         w2_raw = {}
         for a, b, split in W2_LOADS:
-            w2_raw[a] = raw.tile([P, 2 * (b - a), 4, N], F32, name="raw")
+            if a == Y_AFTER:
+                w2_raw[a] = keep.tile([P, 2 * (b - a), 4, N], F32, name="turn", align_bytes=64)
+            else:
+                w2_raw[a] = raw.tile([P, 2 * (b - a), 4, N], F32, name="raw", align_bytes=64)
             src = w2[a:b, :, :].rearrange("e (q p j) n -> p (e q) (j n)", p=P, j=4)
             nc.sync.dma_start(out=w2_raw[a][:].rearrange("p q j n -> p q (j n)"), in_=src)
-        gate_t = raw.tile([P, 2, T], F32, name="raw")
+        nc.sync.dma_start(pos1_t[:], pos1)
+        nc.sync.dma_start(pos2_t[:], pos2)
+        gate_t = keep.tile([P, 2, T], F32)
         nc.sync.dma_start(out=gate_t[:], in_=gate.rearrange("r p t -> p r t"))
 
         x_bf = keep.tile([P, T, 4], BF16, align_bytes=64)
@@ -75,13 +76,14 @@ def tile_routed_moe_kernel(tc, xT, w1, w2, gate, offs, pos1, pos2, out):
 
         gathers = {0: (0, 256), 1: (256, 640), 2: (640, 1024)}
 
-        y_all = keep.tile([P, S], F32)
-
         def cast_w1(e, q):
-            grouped = work.tile([P, 4, P, 4], BF16, name="w1_bf", align_bytes=64)
-            src = w1_raw[e, q].rearrange("p j (m u v) -> p u m j v", u=2, v=2)
+            grouped = work.tile([P, 4, P, 4], BF16, name="w1_bf", align_bytes=64, bufs=4)
+            src = w1_raw[e][:, :, q * HALF:(q + 1) * HALF].rearrange("p j (m u v) -> p u m j v", u=2, v=2)
             dst = grouped[:].rearrange("p (u v) m j -> p u m j v", u=2)
-            if q == 0 or e == 0:
+            if q == 0 and e in SHARED:
+                nc.scalar.copy(out=dst[:, 0], in_=src[:, 0])
+                nc.vector.tensor_copy(out=dst[:, 1], in_=src[:, 1])
+            elif q == 0:
                 nc.scalar.copy(out=dst, in_=src)
             else:
                 nc.vector.tensor_copy(out=dst, in_=src)
@@ -94,7 +96,7 @@ def tile_routed_moe_kernel(tc, xT, w1, w2, gate, offs, pos1, pos2, out):
             return words, scales
 
         def cast_w2(a, b, split):
-            grouped = work.tile([P, 2 * (b - a), N, 4], BF16, name="w2_bf", align_bytes=64, bufs=2)
+            grouped = work.tile([P, 2 * (b - a), N, 4], BF16, name="w2_bf", align_bytes=64, bufs=4)
             src = w2_raw[a][:].rearrange("p q j (c i) -> p q c j i", i=4)
             dst = grouped[:].rearrange("p q (c i) j -> p q c j i", i=4)
             if split > 0:
@@ -104,8 +106,8 @@ def tile_routed_moe_kernel(tc, xT, w1, w2, gate, offs, pos1, pos2, out):
             return grouped
 
         def quant_w2(grouped, n):
-            words = work.tile([P, n * N], U32, name="w2_words", align_bytes=64, bufs=2)
-            scales = work.tile([P, n * N], U8, name="w2_scales", align_bytes=64, bufs=2)
+            words = work.tile([P, n * N], U32, name="w2_words", align_bytes=64, bufs=4)
+            scales = work.tile([P, n * N], U8, name="w2_scales", align_bytes=64, bufs=4)
             nc.vector.quantize_mx(out=words[:].bitcast(FP8X4), scales=scales[:], in_=grouped[:].rearrange("p q n j -> p (q n j)"))
             return words, scales
 
@@ -123,59 +125,64 @@ def tile_routed_moe_kernel(tc, xT, w1, w2, gate, offs, pos1, pos2, out):
                 )
             return bank
 
-        def relu(e, banks, h, zero):
-            for q in range(2):
+        def hidden(banks, h):
+            for q in (1, 0):
                 src = banks[q][:].rearrange("p (t n) -> p n t", t=4)
-                if q == 1 and e in (1, 3, 5):
-                    nc.vector.tensor_scalar(out=h[:, e % 2, q], in0=src, scalar1=zero, scalar2=None, op0=MAX)
-                else:
-                    nc.scalar.activation(out=h[:, e % 2, q], in_=src, func=RELU, bias=zero)
-
-        def quant_h(h):
-            words = hold.tile([P, 4 * C], U32, name="h_words", align_bytes=64)
-            scales = hold.tile([P, 4 * C], U8, name="h_scales", align_bytes=64)
-            nc.vector.quantize_mx(out=words[:].bitcast(FP8X4), scales=scales[:], in_=h[:].rearrange("p e q n t -> p (e q n t)"))
+                dst = h[:, q * HALF:(q + 1) * HALF].rearrange("p (n t) -> p n t", t=4)
+                nc.scalar.activation(out=dst, in_=src, func=RELU)
+            words = work.tile([P, 2 * C], U32, name="h_words", align_bytes=64, bufs=E)
+            scales = work.tile([P, 2 * C], U8, name="h_scales", align_bytes=64, bufs=E)
+            nc.vector.quantize_mx(out=words[:].bitcast(FP8X4), scales=scales[:], in_=h)
             return words, scales
 
-        def layer2(e, w, first, hq):
-            bank = ps_y.tile([P, C], F32, name="y_bank")
+        def layer2(bank, col, w, first, hq):
             for q in range(2):
                 cols = slice((first + q) * N, (first + q + 1) * N)
-                slots = slice((2 * (e % 2) + q) * C, (2 * (e % 2) + q + 1) * C)
+                slots = slice(q * C, (q + 1) * C)
                 nc.tensor.matmul_mx(
-                    out=bank[:],
+                    out=bank[:, col:col + C],
                     lhsT=w[0][:, cols].bitcast(FP8X4), lhsT_scale=w[1][:, cols],
                     rhs=hq[0][:, slots].bitcast(FP8X4), rhs_scale=hq[1][:, slots],
                     start=(q == 0), stop=(q == 1),
                 )
-            nc.scalar.copy(out=y_all[:, e * C:(e + 1) * C], in_=bank[:])
 
         h_codes = []
         banks = {}
-        h = None
         for e in range(E):
             if e in gathers:
                 gather(*gathers[e])
-            halves = [cast_w1(e, q) for q in range(2)]
-            if e > 0:
-                zero = work.tile([P, 1], F32, name="zero")
-                nc.gpsimd.tensor_scalar(out=zero[:], in0=halves[1][:, 3, P - 1, 3:4], scalar1=0.0, scalar2=None, op0=MULT)
-                if e % 2 == 1:
-                    h = work.tile([P, 2, 2, C, 4], BF16, name="h_bf", align_bytes=64, bufs=2)
-                relu(e - 1, banks, h, zero[:])
-                if e % 2 == 0:
-                    h_codes.append(quant_h(h))
+            halves = {q: cast_w1(e, q) for q in (1, 0)}
+            prev = banks
             banks = {}
             for q in (1, 0):
                 banks[q] = layer1(e, quant_w1(halves[q]))
-        relu(E - 1, banks, h, 0.0)
-        for a, b, split in W2_LOADS:
-            g = cast_w2(a, b, split)
-            if a == 0:
-                h_codes.append(quant_h(h))
-            w = quant_w2(g, 2 * (b - a))
+            if 0 < e <= TIED:
+                h_codes.append(hidden(prev, w1_raw[e][:, 3, HALF:H].bitcast(BF16)))
+            if TIED <= e < E - 1:
+                h_own = work.tile([P, H], BF16, name="h_own", align_bytes=64, bufs=2)
+                h_codes.append(hidden(banks, h_own[:]))
+        full = []
+        y_bank = {}
+        for a, b in Y_BANKS:
+            bank = ps_y.tile([P, (b - a) * C], F32, name="y_bank")
             for e in range(a, b):
-                layer2(e, w, 2 * (e - a), h_codes[e // 2])
+                y_bank[e] = (bank, a, b)
+        for a, b, split in W2_LOADS:
+            grouped = cast_w2(a, b, split)
+            if a == Y_AFTER:
+                y_all = keep.tile([P, S], F32, name="turn", align_bytes=64)
+            w = quant_w2(grouped, 2 * (b - a))
+            if a == H_LAST_IN:
+                h_codes.append(hidden(banks, w2_raw[a][:, 0].rearrange("p j n -> p (j n)").bitcast(BF16)))
+            for e in range(a, b):
+                bank, lo, hi = y_bank[e]
+                layer2(bank, (e - lo) * C, w, 2 * (e - a), h_codes[e])
+                if e == hi - 1:
+                    full.append((bank, lo, hi))
+            if a >= Y_AFTER:
+                for bank, lo, hi in full:
+                    nc.scalar.copy(out=y_all[:, lo * C:hi * C], in_=bank[:])
+                full = []
 
         part1 = keep.tile([P, T], F32)
         part2 = keep.tile([P, T], F32)

@@ -15,11 +15,10 @@ P = 128
 K, T, E, C, H, N = 512, 512, 8, 128, 1024, 128
 S = E * C
 HALF = 512
-W2_LOADS = ((0, 2, 2), (2, 4, 2), (4, 6, 2), (6, 7, 0), (7, 8, 1))
+W2_LOADS = ((0, 2, 2), (2, 4, 2), (4, 6, 2), (6, 7, 0))
 Y_BANKS = ((0, 4), (4, 7), (7, 8))
 SHARED = (6,)
 TIED = 6
-Y_AFTER = 7
 H_LAST_IN = 0
 FLOPS = 2 * S * K * H + 2 * S * H * N
 
@@ -46,12 +45,14 @@ def tile_routed_moe_kernel(tc, xT, w1, w2, gate, offs, pos1, pos2, out):
             w1_raw.append(tile)
         w2_raw = {}
         for a, b, split in W2_LOADS:
-            if a == Y_AFTER:
-                w2_raw[a] = keep.tile([P, 2 * (b - a), 4, N], F32, name="turn", align_bytes=64)
-            else:
-                w2_raw[a] = raw.tile([P, 2 * (b - a), 4, N], F32, name="raw", align_bytes=64)
+            w2_raw[a] = raw.tile([P, 2 * (b - a), 4, N], F32, name="raw", align_bytes=64)
             src = w2[a:b, :, :].rearrange("e (q p j) n -> p (e q) (j n)", p=P, j=4)
             nc.sync.dma_start(out=w2_raw[a][:].rearrange("p q j n -> p q (j n)"), in_=src)
+        last_raw = []
+        for q in range(2):
+            tile = keep.tile([P, 4, N], F32, name="turn" if q == 0 else "last_raw", align_bytes=64)
+            nc.sync.dma_start(out=tile[:], in_=w2[E - 1, q * HALF:(q + 1) * HALF, :].rearrange("(p j) n -> p j n", j=4))
+            last_raw.append(tile)
         nc.sync.dma_start(pos1_t[:], pos1)
         nc.sync.dma_start(pos2_t[:], pos2)
         gate_t = keep.tile([P, 2, T], F32)
@@ -169,8 +170,6 @@ def tile_routed_moe_kernel(tc, xT, w1, w2, gate, offs, pos1, pos2, out):
                 y_bank[e] = (bank, a, b)
         for a, b, split in W2_LOADS:
             grouped = cast_w2(a, b, split)
-            if a == Y_AFTER:
-                y_all = keep.tile([P, S], F32, name="turn", align_bytes=64)
             w = quant_w2(grouped, 2 * (b - a))
             if a == H_LAST_IN:
                 h_codes.append(hidden(banks, w2_raw[a][:, 0].rearrange("p j n -> p (j n)").bitcast(BF16)))
@@ -179,15 +178,37 @@ def tile_routed_moe_kernel(tc, xT, w1, w2, gate, offs, pos1, pos2, out):
                 layer2(bank, (e - lo) * C, w, 2 * (e - a), h_codes[e])
                 if e == hi - 1:
                     full.append((bank, lo, hi))
-            if a >= Y_AFTER:
-                for bank, lo, hi in full:
-                    nc.scalar.copy(out=y_all[:, lo * C:hi * C], in_=bank[:])
-                full = []
+
+        bank, lo, hi = y_bank[E - 1]
+        for q in range(2):
+            grouped = work.tile([P, 1, N, 4], BF16, name="w2_bf", align_bytes=64, bufs=4)
+            src = last_raw[q][:].rearrange("p j (c i) -> p c j i", i=4)
+            dst = grouped[:, 0].rearrange("p (c i) j -> p c j i", i=4)
+            if q == 0:
+                nc.scalar.copy(out=dst, in_=src)
+            else:
+                nc.vector.tensor_copy(out=dst, in_=src)
+            words, scales = quant_w2(grouped, 1)
+            slots = slice(q * C, (q + 1) * C)
+            nc.tensor.matmul_mx(
+                out=bank[:],
+                lhsT=words[:].bitcast(FP8X4), lhsT_scale=scales[:],
+                rhs=h_codes[E - 1][0][:, slots].bitcast(FP8X4), rhs_scale=h_codes[E - 1][1][:, slots],
+                start=(q == 0), stop=(q == 1),
+            )
+        y_all = keep.tile([P, S], F32, name="turn", align_bytes=64)
+        full.append((bank, lo, hi))
+        for bank, lo, hi in full:
+            nc.scalar.copy(out=y_all[:, lo * C:hi * C], in_=bank[:])
 
         part1 = keep.tile([P, T], F32)
-        part2 = keep.tile([P, T], F32)
-        result = keep.tile([P, T], F32)
         nc.vector.tensor_tensor(part1[:], y_all[:].indirect(pos1_t[:]), gate_t[:, 0, :], MULT)
-        nc.vector.tensor_tensor(part2[:], y_all[:].indirect(pos2_t[:]), gate_t[:, 1, :], MULT)
-        nc.vector.tensor_add(result[:], part1[:], part2[:])
-        nc.sync.dma_start(out=out, in_=result[:])
+        pieces = ((0, 256), (256, T))
+        part2 = {}
+        for a, b in pieces:
+            part2[a] = keep.tile([P, b - a], F32, name="part2_%d" % a)
+            nc.vector.tensor_tensor(part2[a][:], y_all[:].indirect(pos2_t[:, a // 16:b // 16]), gate_t[:, 1, a:b], MULT)
+        for a, b in pieces:
+            result = keep.tile([P, b - a], F32, name="result_%d" % a)
+            nc.vector.tensor_add(result[:], part1[:, a:b], part2[a][:])
+            nc.sync.dma_start(out=out[:, a:b], in_=result[:])

@@ -15,7 +15,7 @@ P = 128
 K, T, E, C, H, N = 512, 512, 8, 128, 1024, 128
 S = E * C
 HALF = 512
-W2_LOADS = ((0, 2, 2), (2, 4, 2), (4, 6, 2), (6, 7, 0))
+W2_LOADS = ((0, 4), (4, 8), (8, 12), (12, 15))
 Y_BANKS = ((0, 4), (4, 7), (7, 8))
 SHARED = (6,)
 TIED = 6
@@ -43,20 +43,19 @@ def tile_routed_moe_kernel(tc, xT, w1, w2, gate, offs, pos1, pos2, out):
             tile = raw.tile([P, 4, H], F32, name="raw", align_bytes=64)
             nc.sync.dma_start(out=tile[:], in_=w1[e].rearrange("(p j) c -> p j c", j=4))
             w1_raw.append(tile)
+        w2_passes = w2.rearrange("e (q p j) n -> p (e q) (j n)", p=P, j=4)
         w2_raw = {}
-        for a, b, split in W2_LOADS:
-            w2_raw[a] = raw.tile([P, 2 * (b - a), 4, N], F32, name="raw", align_bytes=64)
-            src = w2[a:b, :, :].rearrange("e (q p j) n -> p (e q) (j n)", p=P, j=4)
-            nc.sync.dma_start(out=w2_raw[a][:].rearrange("p q j n -> p q (j n)"), in_=src)
-        last_raw = []
-        for q in range(2):
-            tile = keep.tile([P, 4, N], F32, name="turn" if q == 0 else "last_raw", align_bytes=64)
-            nc.sync.dma_start(out=tile[:], in_=w2[E - 1, q * HALF:(q + 1) * HALF, :].rearrange("(p j) n -> p j n", j=4))
-            last_raw.append(tile)
-        nc.sync.dma_start(pos1_t[:], pos1)
-        nc.sync.dma_start(pos2_t[:], pos2)
-        gate_t = keep.tile([P, 2, T], F32)
-        nc.sync.dma_start(out=gate_t[:], in_=gate.rearrange("r p t -> p r t"))
+        for a, b in W2_LOADS:
+            w2_raw[a] = raw.tile([P, b - a, 4, N], F32, name="raw", align_bytes=64)
+            nc.sync.dma_start(out=w2_raw[a][:].rearrange("p q j n -> p q (j n)"), in_=w2_passes[:, a:b])
+        last_raw = keep.tile([P, 1, 4, N], F32, name="turn", align_bytes=64)
+        nc.sync.dma_start(out=last_raw[:].rearrange("p q j n -> p q (j n)"), in_=w2_passes[:, 2 * E - 1:2 * E])
+        gate_t = []
+        for r, (pos_t, pos) in enumerate(((pos1_t, pos1), (pos2_t, pos2))):
+            tile = keep.tile([P, T], F32, name="gate_%d" % r)
+            nc.sync.dma_start(out=tile[:], in_=gate[r])
+            nc.sync.dma_start(pos_t[:], pos)
+            gate_t.append(tile)
 
         x_bf = keep.tile([P, T, 4], BF16, align_bytes=64)
         x_words = keep.tile([P, T], U32, align_bytes=64)
@@ -96,14 +95,14 @@ def tile_routed_moe_kernel(tc, xT, w1, w2, gate, offs, pos1, pos2, out):
             nc.vector.quantize_mx(out=words[:].bitcast(FP8X4), scales=scales[:], in_=grouped[:].rearrange("p t m j -> p (t m j)"))
             return words, scales
 
-        def cast_w2(a, b, split):
-            grouped = work.tile([P, 2 * (b - a), N, 4], BF16, name="w2_bf", align_bytes=64, bufs=4)
-            src = w2_raw[a][:].rearrange("p q j (c i) -> p q c j i", i=4)
+        def cast_w2(tile, a, b, on_vector):
+            grouped = work.tile([P, b - a, N, 4], BF16, name="w2_bf", align_bytes=64, bufs=4)
+            src = tile[:, a:b].rearrange("p q j (c i) -> p q c j i", i=4)
             dst = grouped[:].rearrange("p q (c i) j -> p q c j i", i=4)
-            if split > 0:
-                nc.vector.tensor_copy(out=dst[:, 0:split], in_=src[:, 0:split])
-            if split < 2 * (b - a):
-                nc.scalar.copy(out=dst[:, split:], in_=src[:, split:])
+            if on_vector:
+                nc.vector.tensor_copy(out=dst, in_=src)
+            else:
+                nc.scalar.copy(out=dst, in_=src)
             return grouped
 
         def quant_w2(grouped, n):
@@ -136,16 +135,17 @@ def tile_routed_moe_kernel(tc, xT, w1, w2, gate, offs, pos1, pos2, out):
             nc.vector.quantize_mx(out=words[:].bitcast(FP8X4), scales=scales[:], in_=h)
             return words, scales
 
-        def layer2(bank, col, w, first, hq):
-            for q in range(2):
-                cols = slice((first + q) * N, (first + q + 1) * N)
-                slots = slice(q * C, (q + 1) * C)
-                nc.tensor.matmul_mx(
-                    out=bank[:, col:col + C],
-                    lhsT=w[0][:, cols].bitcast(FP8X4), lhsT_scale=w[1][:, cols],
-                    rhs=hq[0][:, slots].bitcast(FP8X4), rhs_scale=hq[1][:, slots],
-                    start=(q == 0), stop=(q == 1),
-                )
+        def layer2(g, w, first):
+            e, q = divmod(g, 2)
+            bank, lo, hi = y_bank[e]
+            cols = slice((g - first) * N, (g - first + 1) * N)
+            slots = slice(q * C, (q + 1) * C)
+            nc.tensor.matmul_mx(
+                out=bank[:, (e - lo) * C:(e - lo + 1) * C],
+                lhsT=w[0][:, cols].bitcast(FP8X4), lhsT_scale=w[1][:, cols],
+                rhs=h_codes[e][0][:, slots].bitcast(FP8X4), rhs_scale=h_codes[e][1][:, slots],
+                start=(q == 0), stop=(q == 1),
+            )
 
         h_codes = []
         banks = {}
@@ -162,52 +162,35 @@ def tile_routed_moe_kernel(tc, xT, w1, w2, gate, offs, pos1, pos2, out):
             if TIED <= e < E - 1:
                 h_own = work.tile([P, H], BF16, name="h_own", align_bytes=64, bufs=2)
                 h_codes.append(hidden(banks, h_own[:]))
-        full = []
         y_bank = {}
         for a, b in Y_BANKS:
             bank = ps_y.tile([P, (b - a) * C], F32, name="y_bank")
             for e in range(a, b):
                 y_bank[e] = (bank, a, b)
-        for a, b, split in W2_LOADS:
-            grouped = cast_w2(a, b, split)
-            w = quant_w2(grouped, 2 * (b - a))
+        for a, b in W2_LOADS:
+            shares = [(0, 2, cast_w2(w2_raw[a], 0, 2, True)), (2, b - a, cast_w2(w2_raw[a], 2, b - a, False))]
+            codes = [(lo, hi, quant_w2(grouped, hi - lo)) for lo, hi, grouped in shares]
             if a == H_LAST_IN:
                 h_codes.append(hidden(banks, w2_raw[a][:, 0].rearrange("p j n -> p (j n)").bitcast(BF16)))
-            for e in range(a, b):
-                bank, lo, hi = y_bank[e]
-                layer2(bank, (e - lo) * C, w, 2 * (e - a), h_codes[e])
-                if e == hi - 1:
-                    full.append((bank, lo, hi))
+            for lo, hi, w in codes:
+                for g in range(a + lo, a + hi):
+                    layer2(g, w, a + lo)
+        layer2(2 * E - 1, quant_w2(cast_w2(last_raw, 0, 1, False), 1), 2 * E - 1)
 
-        bank, lo, hi = y_bank[E - 1]
-        for q in range(2):
-            grouped = work.tile([P, 1, N, 4], BF16, name="w2_bf", align_bytes=64, bufs=4)
-            src = last_raw[q][:].rearrange("p j (c i) -> p c j i", i=4)
-            dst = grouped[:, 0].rearrange("p (c i) j -> p c j i", i=4)
-            if q == 0:
-                nc.scalar.copy(out=dst, in_=src)
-            else:
-                nc.vector.tensor_copy(out=dst, in_=src)
-            words, scales = quant_w2(grouped, 1)
-            slots = slice(q * C, (q + 1) * C)
-            nc.tensor.matmul_mx(
-                out=bank[:],
-                lhsT=words[:].bitcast(FP8X4), lhsT_scale=scales[:],
-                rhs=h_codes[E - 1][0][:, slots].bitcast(FP8X4), rhs_scale=h_codes[E - 1][1][:, slots],
-                start=(q == 0), stop=(q == 1),
-            )
         y_all = keep.tile([P, S], F32, name="turn", align_bytes=64)
-        full.append((bank, lo, hi))
-        for bank, lo, hi in full:
-            nc.scalar.copy(out=y_all[:, lo * C:hi * C], in_=bank[:])
+        for k, (lo, hi) in enumerate(Y_BANKS):
+            if k == 1:
+                nc.vector.tensor_copy(out=y_all[:, lo * C:hi * C], in_=y_bank[lo][0][:])
+            else:
+                nc.scalar.copy(out=y_all[:, lo * C:hi * C], in_=y_bank[lo][0][:])
 
         part1 = keep.tile([P, T], F32)
-        nc.vector.tensor_tensor(part1[:], y_all[:].indirect(pos1_t[:]), gate_t[:, 0, :], MULT)
+        nc.vector.tensor_tensor(part1[:], y_all[:].indirect(pos1_t[:]), gate_t[0][:], MULT)
         pieces = ((0, 256), (256, T))
         part2 = {}
         for a, b in pieces:
             part2[a] = keep.tile([P, b - a], F32, name="part2_%d" % a)
-            nc.vector.tensor_tensor(part2[a][:], y_all[:].indirect(pos2_t[:, a // 16:b // 16]), gate_t[:, 1, a:b], MULT)
+            nc.vector.tensor_tensor(part2[a][:], y_all[:].indirect(pos2_t[:, a // 16:b // 16]), gate_t[1][:, a:b], MULT)
         for a, b in pieces:
             result = keep.tile([P, b - a], F32, name="result_%d" % a)
             nc.vector.tensor_add(result[:], part1[:, a:b], part2[a][:])

@@ -15,7 +15,7 @@ P = 128
 K, T, E, C, H, N = 512, 512, 8, 128, 1024, 128
 S = E * C
 HALF = 512
-W2_LOADS = ((0, 4), (4, 8), (8, 12), (12, 15))
+W2_LOADS = ((0, 4), (4, 8), (8, 12), (12, 14))
 Y_BANKS = ((0, 4), (4, 7), (7, 8))
 SHARED = (6,)
 TIED = 6
@@ -48,8 +48,11 @@ def tile_routed_moe_kernel(tc, xT, w1, w2, gate, offs, pos1, pos2, out):
         for a, b in W2_LOADS:
             w2_raw[a] = raw.tile([P, b - a, 4, N], F32, name="raw", align_bytes=64)
             nc.sync.dma_start(out=w2_raw[a][:].rearrange("p q j n -> p q (j n)"), in_=w2_passes[:, a:b])
-        last_raw = keep.tile([P, 1, 4, N], F32, name="turn", align_bytes=64)
-        nc.sync.dma_start(out=last_raw[:].rearrange("p q j n -> p q (j n)"), in_=w2_passes[:, 2 * E - 1:2 * E])
+        last_raw = []
+        for q in range(2):
+            tile = keep.tile([P, 1, 4, N], F32, name="turn_%d" % q, align_bytes=64)
+            nc.sync.dma_start(out=tile[:].rearrange("p q j n -> p q (j n)"), in_=w2_passes[:, 2 * E - 2 + q:2 * E - 1 + q])
+            last_raw.append(tile)
         gate_t = []
         for r, (pos_t, pos) in enumerate(((pos1_t, pos1), (pos2_t, pos2))):
             tile = keep.tile([P, T], F32, name="gate_%d" % r)
@@ -95,20 +98,23 @@ def tile_routed_moe_kernel(tc, xT, w1, w2, gate, offs, pos1, pos2, out):
             nc.vector.quantize_mx(out=words[:].bitcast(FP8X4), scales=scales[:], in_=grouped[:].rearrange("p t m j -> p (t m j)"))
             return words, scales
 
-        def cast_w2(tile, a, b, on_vector):
-            grouped = work.tile([P, b - a, N, 4], BF16, name="w2_bf", align_bytes=64, bufs=4)
+        def cast_w2(tile, a, b, on_vector, grouped=None):
+            if grouped is None:
+                fresh = work.tile([P, (b - a) * HALF], BF16, name="w2_bf", align_bytes=64, bufs=6)
+                grouped = fresh[:]
             src = tile[:, a:b].rearrange("p q j (c i) -> p q c j i", i=4)
-            dst = grouped[:].rearrange("p q (c i) j -> p q c j i", i=4)
+            dst = grouped.rearrange("p (q c i j) -> p q c j i", q=b - a, i=4, j=4)
             if on_vector:
                 nc.vector.tensor_copy(out=dst, in_=src)
             else:
                 nc.scalar.copy(out=dst, in_=src)
             return grouped
 
-        def quant_w2(grouped, n):
-            words = work.tile([P, n * N], U32, name="w2_words", align_bytes=64, bufs=4)
-            scales = work.tile([P, n * N], U8, name="w2_scales", align_bytes=64, bufs=4)
-            nc.vector.quantize_mx(out=words[:].bitcast(FP8X4), scales=scales[:], in_=grouped[:].rearrange("p q n j -> p (q n j)"))
+        def quant_w2(grouped, n, words=None):
+            if words is None:
+                words = work.tile([P, n * N], U32, name="w2_words", align_bytes=64, bufs=8)
+            scales = work.tile([P, n * N], U8, name="w2_scales", align_bytes=64, bufs=8)
+            nc.vector.quantize_mx(out=words[:].bitcast(FP8X4), scales=scales[:], in_=grouped)
             return words, scales
 
         def layer1(e, w):
@@ -125,25 +131,26 @@ def tile_routed_moe_kernel(tc, xT, w1, w2, gate, offs, pos1, pos2, out):
                 )
             return bank
 
+        def relu(bank, h):
+            src = bank[:].rearrange("p (t n) -> p n t", t=4)
+            nc.scalar.activation(out=h.rearrange("p (n t) -> p n t", t=4), in_=src, func=RELU)
+
         def hidden(banks, h):
             for q in (1, 0):
-                src = banks[q][:].rearrange("p (t n) -> p n t", t=4)
-                dst = h[:, q * HALF:(q + 1) * HALF].rearrange("p (n t) -> p n t", t=4)
-                nc.scalar.activation(out=dst, in_=src, func=RELU)
+                relu(banks[q], h[:, q * HALF:(q + 1) * HALF])
             words = work.tile([P, 2 * C], U32, name="h_words", align_bytes=64, bufs=E)
             scales = work.tile([P, 2 * C], U8, name="h_scales", align_bytes=64, bufs=E)
             nc.vector.quantize_mx(out=words[:].bitcast(FP8X4), scales=scales[:], in_=h)
-            return words, scales
+            return [(words, scales, q * C) for q in range(2)]
 
-        def layer2(g, w, first):
+        def layer2(g, w, col):
             e, q = divmod(g, 2)
             bank, lo, hi = y_bank[e]
-            cols = slice((g - first) * N, (g - first + 1) * N)
-            slots = slice(q * C, (q + 1) * C)
+            h_words, h_scales, h_col = h_codes[e][q]
             nc.tensor.matmul_mx(
                 out=bank[:, (e - lo) * C:(e - lo + 1) * C],
-                lhsT=w[0][:, cols].bitcast(FP8X4), lhsT_scale=w[1][:, cols],
-                rhs=h_codes[e][0][:, slots].bitcast(FP8X4), rhs_scale=h_codes[e][1][:, slots],
+                lhsT=w[0][:, col:col + N].bitcast(FP8X4), lhsT_scale=w[1][:, col:col + N],
+                rhs=h_words[:, h_col:h_col + C].bitcast(FP8X4), rhs_scale=h_scales[:, h_col:h_col + C],
                 start=(q == 0), stop=(q == 1),
             )
 
@@ -167,22 +174,39 @@ def tile_routed_moe_kernel(tc, xT, w1, w2, gate, offs, pos1, pos2, out):
             bank = ps_y.tile([P, (b - a) * C], F32, name="y_bank")
             for e in range(a, b):
                 y_bank[e] = (bank, a, b)
-        for a, b in W2_LOADS:
-            shares = [(0, 2, cast_w2(w2_raw[a], 0, 2, True)), (2, b - a, cast_w2(w2_raw[a], 2, b - a, False))]
-            codes = [(lo, hi, quant_w2(grouped, hi - lo)) for lo, hi, grouped in shares]
-            if a == H_LAST_IN:
-                h_codes.append(hidden(banks, w2_raw[a][:, 0].rearrange("p j n -> p (j n)").bitcast(BF16)))
-            for lo, hi, w in codes:
-                for g in range(a + lo, a + hi):
-                    layer2(g, w, a + lo)
-        layer2(2 * E - 1, quant_w2(cast_w2(last_raw, 0, 1, False), 1), 2 * E - 1)
-
-        y_all = keep.tile([P, S], F32, name="turn", align_bytes=64)
-        for k, (lo, hi) in enumerate(Y_BANKS):
-            if k == 1:
-                nc.vector.tensor_copy(out=y_all[:, lo * C:hi * C], in_=y_bank[lo][0][:])
+        joint = [w2_raw[0][:, 2 + q].rearrange("p j n -> p (j n)").bitcast(BF16) for q in range(2)]
+        for a, b in W2_LOADS[:3]:
+            own = [cast_w2(w2_raw[a], k, k + 1, True, joint[k][:, HALF:] if a == 4 else None) for k in range(2)]
+            other = cast_w2(w2_raw[a], 2, 4, False)
+            if a == 0:
+                for q in (1, 0):
+                    relu(banks[q], joint[q][:, :HALF])
+            if a == 4:
+                codes = [quant_w2(joint[k], 2) for k in range(2)]
+                h_codes.append([(codes[q][0], codes[q][1], 0) for q in range(2)])
+                for k in range(2):
+                    layer2(a + k, codes[k], N)
             else:
-                nc.scalar.copy(out=y_all[:, lo * C:hi * C], in_=y_bank[lo][0][:])
+                codes = [quant_w2(own[k], 1) for k in range(2)]
+                for k in range(2):
+                    layer2(a + k, codes[k], 0)
+            codes = quant_w2(other, 2)
+            for k in range(2):
+                layer2(a + 2 + k, codes, k * N)
+        both = work.tile([P, 2 * HALF], BF16, name="w2_bf", align_bytes=64, bufs=6)
+        for k in range(2):
+            cast_w2(w2_raw[12], k, k + 1, k == 0, both[:, k * HALF:(k + 1) * HALF])
+        codes = quant_w2(both[:], 2)
+        for k in range(2):
+            layer2(12 + k, codes, k * N)
+        last_bf = [cast_w2(last_raw[q], 0, 1, q == 1) for q in range(2)]
+        tied_words = keep.tile([P, N], U32, name="turn_1", align_bytes=64)
+        layer2(2 * E - 2, quant_w2(last_bf[0], 1, tied_words), 0)
+        layer2(2 * E - 1, quant_w2(last_bf[1], 1), 0)
+
+        y_all = keep.tile([P, S], F32, name="turn_0", align_bytes=64)
+        for lo, hi in Y_BANKS:
+            nc.scalar.copy(out=y_all[:, lo * C:hi * C], in_=y_bank[lo][0][:])
 
         part1 = keep.tile([P, T], F32)
         nc.vector.tensor_tensor(part1[:], y_all[:].indirect(pos1_t[:]), gate_t[0][:], MULT)

@@ -35,27 +35,27 @@ def tile_routed_moe_kernel(tc, xT, w1, w2, gate, offs, pos1, pos2, out):
         offs_t = keep.tile([P, S // 16], U16)
         pos1_t = keep.tile([P, T // 16], U16)
         pos2_t = keep.tile([P, T // 16], U16)
-        x_raw = keep.tile([P, 4, T], F32)
+        x_raw = keep.tile([P, 4, T], F32, align_bytes=256)
         nc.sync.dma_start(out=x_raw[:], in_=xT.rearrange("(p j) t -> p j t", j=4))
         nc.sync.dma_start(offs_t[:], offs)
         w1_raw = []
         for e in range(E):
-            tile = raw.tile([P, 4, H], F32, name="raw", align_bytes=64)
+            tile = raw.tile([P, 4, H], F32, name="raw", align_bytes=256)
             nc.sync.dma_start(out=tile[:], in_=w1[e].rearrange("(p j) c -> p j c", j=4))
             w1_raw.append(tile)
         w2_passes = w2.rearrange("e (q p j) n -> p (e q) (j n)", p=P, j=4)
         w2_raw = {}
         for a, b in W2_LOADS:
-            w2_raw[a] = raw.tile([P, b - a, 4, N], F32, name="raw", align_bytes=64)
+            w2_raw[a] = raw.tile([P, b - a, 4, N], F32, name="raw", align_bytes=256)
             nc.sync.dma_start(out=w2_raw[a][:].rearrange("p q j n -> p q (j n)"), in_=w2_passes[:, a:b])
         last_raw = []
         for q in range(2):
-            tile = keep.tile([P, 1, 4, N], F32, name="turn_%d" % q, align_bytes=64)
+            tile = keep.tile([P, 1, 4, N], F32, name="turn_%d" % q, align_bytes=256)
             nc.sync.dma_start(out=tile[:].rearrange("p q j n -> p q (j n)"), in_=w2_passes[:, 2 * E - 2 + q:2 * E - 1 + q])
             last_raw.append(tile)
         gate_t = []
         for r, (pos_t, pos) in enumerate(((pos1_t, pos1), (pos2_t, pos2))):
-            tile = keep.tile([P, T], F32, name="gate_%d" % r)
+            tile = keep.tile([P, T], F32, name="gate_%d" % r, align_bytes=256)
             nc.sync.dma_start(out=tile[:], in_=gate[r])
             nc.sync.dma_start(pos_t[:], pos)
             gate_t.append(tile)
@@ -200,11 +200,11 @@ def tile_routed_moe_kernel(tc, xT, w1, w2, gate, offs, pos1, pos2, out):
         for k in range(2):
             layer2(12 + k, codes, k * N)
         last_bf = [cast_w2(last_raw[q], 0, 1, q == 1) for q in range(2)]
-        tied_words = keep.tile([P, N], U32, name="turn_1", align_bytes=64)
+        tied_words = keep.tile([P, N], U32, name="turn_1", align_bytes=256)
         layer2(2 * E - 2, quant_w2(last_bf[0], 1, tied_words), 0)
         layer2(2 * E - 1, quant_w2(last_bf[1], 1), 0)
 
-        y_all = keep.tile([P, S], F32, name="turn_0", align_bytes=64)
+        y_all = keep.tile([P, S], F32, name="turn_0", align_bytes=256)
         for lo, hi in Y_BANKS:
             nc.scalar.copy(out=y_all[:, lo * C:hi * C], in_=y_bank[lo][0][:])
 
@@ -216,6 +216,6 @@ def tile_routed_moe_kernel(tc, xT, w1, w2, gate, offs, pos1, pos2, out):
             part2[a] = keep.tile([P, b - a], F32, name="part2_%d" % a)
             nc.vector.tensor_tensor(part2[a][:], y_all[:].indirect(pos2_t[:, a // 16:b // 16]), gate_t[1][:, a:b], MULT)
         for a, b in pieces:
-            result = keep.tile([P, b - a], F32, name="result_%d" % a)
+            result = keep.tile([P, b - a], F32, name="result_%d" % a, align_bytes=256)
             nc.vector.tensor_add(result[:], part1[:, a:b], part2[a][:])
             nc.sync.dma_start(out=out[:, a:b], in_=result[:])

@@ -32,9 +32,9 @@ def tile_routed_moe_kernel(tc, xT, w1, w2, gate, offs, pos1, pos2, out):
         ps_a = ctx.enter_context(tc.psum_pool(name="ps_a", bufs=5))
         ps_y = ctx.enter_context(tc.psum_pool(name="ps_y", bufs=3))
 
-        offs_t = keep.tile([P, S // 16], U16)
-        pos1_t = keep.tile([P, T // 16], U16)
-        pos2_t = keep.tile([P, T // 16], U16)
+        offs_t = keep.tile([P, S // 16], U16, align_bytes=128)
+        pos1_t = keep.tile([P, T // 16], U16, align_bytes=64)
+        pos2_t = keep.tile([P, T // 16], U16, align_bytes=64)
         x_raw = keep.tile([P, 4, T], F32, align_bytes=256)
         nc.sync.dma_start(out=x_raw[:], in_=xT.rearrange("(p j) t -> p j t", j=4))
         nc.sync.dma_start(offs_t[:], offs)
@@ -79,24 +79,23 @@ def tile_routed_moe_kernel(tc, xT, w1, w2, gate, offs, pos1, pos2, out):
 
         gathers = {0: (0, 256), 1: (256, 640), 2: (640, 1024)}
 
-        def cast_w1(e, q):
-            grouped = work.tile([P, 4, P, 4], BF16, name="w1_bf", align_bytes=64, bufs=4)
+        def cast_w1(e, q, grouped, on_vector, u=None):
             src = w1_raw[e][:, :, q * HALF:(q + 1) * HALF].rearrange("p j (m u v) -> p u m j v", u=2, v=2)
-            dst = grouped[:].rearrange("p (u v) m j -> p u m j v", u=2)
-            if q == 0 and e in SHARED:
-                nc.scalar.copy(out=dst[:, 0], in_=src[:, 0])
-                nc.vector.tensor_copy(out=dst[:, 1], in_=src[:, 1])
-            elif q == 0:
-                nc.scalar.copy(out=dst, in_=src)
+            if u is None:
+                dst = grouped.rearrange("p (u v m j) -> p u m j v", u=2, v=2, j=4)
             else:
+                src = src[:, u]
+                dst = grouped.rearrange("p (v m j) -> p m j v", v=2, j=4)
+            if on_vector:
                 nc.vector.tensor_copy(out=dst, in_=src)
-            return grouped
+            else:
+                nc.scalar.copy(out=dst, in_=src)
 
-        def quant_w1(grouped):
-            words = work.tile([P, HALF], U32, name="w1_words", align_bytes=64, bufs=4)
-            scales = work.tile([P, HALF], U8, name="w1_scales", align_bytes=64, bufs=4)
-            nc.vector.quantize_mx(out=words[:].bitcast(FP8X4), scales=scales[:], in_=grouped[:].rearrange("p t m j -> p (t m j)"))
-            return words, scales
+        def quant_w1(grouped, n):
+            words = work.tile([P, n * P], U32, name="w1_words", align_bytes=64, bufs=5)
+            scales = work.tile([P, n * P], U8, name="w1_scales", align_bytes=64, bufs=5)
+            nc.vector.quantize_mx(out=words[:].bitcast(FP8X4), scales=scales[:], in_=grouped)
+            return [(words, scales, k * P) for k in range(n)]
 
         def cast_w2(tile, a, b, on_vector, grouped=None):
             if grouped is None:
@@ -117,15 +116,13 @@ def tile_routed_moe_kernel(tc, xT, w1, w2, gate, offs, pos1, pos2, out):
             nc.vector.quantize_mx(out=words[:].bitcast(FP8X4), scales=scales[:], in_=grouped)
             return words, scales
 
-        def layer1(e, w):
-            words, scales = w
+        def layer1(e, blocks):
             bank = ps_a.tile([P, 4 * C], F32, name="h_bank")
             slots = slice(e * C, (e + 1) * C)
-            for t in range(4):
-                cols = slice(t * P, (t + 1) * P)
+            for t, (words, scales, col) in enumerate(blocks):
                 nc.tensor.matmul_mx(
                     out=bank[:, t * C:(t + 1) * C],
-                    lhsT=words[:, cols].bitcast(FP8X4), lhsT_scale=scales[:, cols],
+                    lhsT=words[:, col:col + P].bitcast(FP8X4), lhsT_scale=scales[:, col:col + P],
                     rhs=g_words[:, slots].bitcast(FP8X4), rhs_scale=g_bytes[:, slots],
                     start=True, stop=True,
                 )
@@ -156,19 +153,35 @@ def tile_routed_moe_kernel(tc, xT, w1, w2, gate, offs, pos1, pos2, out):
 
         h_codes = []
         banks = {}
-        for e in range(E):
+        for e in range(E - 1):
             if e in gathers:
                 gather(*gathers[e])
-            halves = {q: cast_w1(e, q) for q in (1, 0)}
+            upper = work.tile([P, 4 * HALF], BF16, name="w1_bf", align_bytes=64, bufs=4)
+            lower = work.tile([P, 4 * HALF], BF16, name="w1_bf", align_bytes=64, bufs=4)
+            cast_w1(e, 1, upper[:], True)
+            if e in SHARED:
+                cast_w1(e, 0, lower[:, :H], False, 0)
+                cast_w1(e, 0, lower[:, H:], True, 1)
+            else:
+                cast_w1(e, 0, lower[:], False)
             prev = banks
-            banks = {}
-            for q in (1, 0):
-                banks[q] = layer1(e, quant_w1(halves[q]))
-            if 0 < e <= TIED:
+            banks = {1: layer1(e, quant_w1(upper[:], 4)), 0: layer1(e, quant_w1(lower[:], 4))}
+            if e > 0:
                 h_codes.append(hidden(prev, w1_raw[e][:, 3, HALF:H].bitcast(BF16)))
-            if TIED <= e < E - 1:
-                h_own = work.tile([P, H], BF16, name="h_own", align_bytes=64, bufs=2)
-                h_codes.append(hidden(banks, h_own[:]))
+        first = keep.tile([P, 2 * H], BF16, name="first", align_bytes=64)
+        second = work.tile([P, H], BF16, name="w1_bf", align_bytes=64, bufs=4)
+        lower = work.tile([P, 4 * HALF], BF16, name="w1_bf", align_bytes=64, bufs=4)
+        for q in (1, 0):
+            relu(banks[q], first[:, q * HALF:(q + 1) * HALF])
+        cast_w1(E - 1, 1, first[:, H:], True, 0)
+        cast_w1(E - 1, 1, second[:], True, 1)
+        cast_w1(E - 1, 0, lower[:], False)
+        words = keep.tile([P, HALF], U32, name="first_words", align_bytes=64)
+        scales = keep.tile([P, HALF], U8, name="first_scales", align_bytes=64)
+        nc.vector.quantize_mx(out=words[:].bitcast(FP8X4), scales=scales[:], in_=first[:])
+        blocks = [(words, scales, k * P) for k in range(4)]
+        h_codes.append(blocks[:2])
+        banks = {1: layer1(E - 1, blocks[2:] + quant_w1(second[:], 2)), 0: layer1(E - 1, quant_w1(lower[:], 4))}
         y_bank = {}
         for a, b in Y_BANKS:
             bank = ps_y.tile([P, (b - a) * C], F32, name="y_bank")
@@ -193,20 +206,19 @@ def tile_routed_moe_kernel(tc, xT, w1, w2, gate, offs, pos1, pos2, out):
             codes = quant_w2(other, 2)
             for k in range(2):
                 layer2(a + 2 + k, codes, k * N)
-        both = work.tile([P, 2 * HALF], BF16, name="w2_bf", align_bytes=64, bufs=6)
+        own = [cast_w2(w2_raw[12], k, k + 1, True) for k in range(2)]
+        codes = [quant_w2(own[k], 1) for k in range(2)]
         for k in range(2):
-            cast_w2(w2_raw[12], k, k + 1, k == 0, both[:, k * HALF:(k + 1) * HALF])
-        codes = quant_w2(both[:], 2)
-        for k in range(2):
-            layer2(12 + k, codes, k * N)
-        last_bf = [cast_w2(last_raw[q], 0, 1, q == 1) for q in range(2)]
-        tied_words = keep.tile([P, N], U32, name="turn_1", align_bytes=256)
-        layer2(2 * E - 2, quant_w2(last_bf[0], 1, tied_words), 0)
-        layer2(2 * E - 1, quant_w2(last_bf[1], 1), 0)
+            layer2(12 + k, codes[k], 0)
+        for q in range(2):
+            layer2(2 * E - 2 + q, quant_w2(cast_w2(last_raw[q], 0, 1, False), 1), 0)
 
-        y_all = keep.tile([P, S], F32, name="turn_0", align_bytes=256)
-        for lo, hi in Y_BANKS:
-            nc.scalar.copy(out=y_all[:, lo * C:hi * C], in_=y_bank[lo][0][:])
+        y_all = keep.tile([P, S], F32, name="turn_1", align_bytes=256)
+        for k, (lo, hi) in enumerate(Y_BANKS):
+            if k == 1:
+                nc.vector.tensor_copy(out=y_all[:, lo * C:hi * C], in_=y_bank[lo][0][:])
+            else:
+                nc.scalar.copy(out=y_all[:, lo * C:hi * C], in_=y_bank[lo][0][:])
 
         part1 = keep.tile([P, T], F32)
         nc.vector.tensor_tensor(part1[:], y_all[:].indirect(pos1_t[:]), gate_t[0][:], MULT)

@@ -210,8 +210,13 @@ def tile_routed_moe_kernel(tc, xT, w1, w2, gate, offs, pos1, pos2, out):
         codes = [quant_w2(own[k], 1) for k in range(2)]
         for k in range(2):
             layer2(12 + k, codes[k], 0)
-        for q in range(2):
-            layer2(2 * E - 2 + q, quant_w2(cast_w2(last_raw[q], 0, 1, False), 1), 0)
+        layer2(2 * E - 2, quant_w2(cast_w2(last_raw[0], 0, 1, False), 1), 0)
+        final = work.tile([P, HALF], BF16, name="w2_bf", align_bytes=64, bufs=6)
+        src = last_raw[1][:, 0].rearrange("p j (c i) -> p c j i", i=4)
+        dst = final[:].rearrange("p (c i j) -> p c j i", i=4, j=4)
+        nc.scalar.copy(out=dst[:, :16], in_=src[:, :16])
+        nc.vector.tensor_copy(out=dst[:, 16:], in_=src[:, 16:])
+        layer2(2 * E - 1, quant_w2(final[:], 1), 0)
 
         y_all = keep.tile([P, S], F32, name="turn_1", align_bytes=256)
         for k, (lo, hi) in enumerate(Y_BANKS):

@@ -17,9 +17,8 @@ S = E * C
 HALF = 512
 W2_LOADS = ((0, 4), (4, 8), (8, 12), (12, 14))
 Y_BANKS = ((0, 4), (4, 7), (7, 8))
-SHARED = (6,)
-TIED = 6
-H_LAST_IN = 0
+W1_LOADS = ((0, 2), (2, 4), (4, 5), (5, 6), (6, 7), (7, 8))
+SHARED = (3, 4, 6)
 FLOPS = 2 * S * K * H + 2 * S * H * N
 
 
@@ -39,14 +38,16 @@ def tile_routed_moe_kernel(tc, xT, w1, w2, gate, offs, pos1, pos2, out):
         nc.sync.dma_start(out=x_raw[:], in_=xT.rearrange("(p j) t -> p j t", j=4))
         nc.sync.dma_start(offs_t[:], offs)
         w1_raw = []
-        for e in range(E):
-            tile = raw.tile([P, 4, H], F32, name="raw", align_bytes=256)
-            nc.sync.dma_start(out=tile[:], in_=w1[e].rearrange("(p j) c -> p j c", j=4))
-            w1_raw.append(tile)
+        w1_rows = w1.rearrange("e (p j) c -> p e (j c)", j=4)
+        for a, b in W1_LOADS:
+            tile = raw.tile([P, b - a, 4, H], F32, name="raw_%d" % (b - a), align_bytes=256, bufs=4 // (b - a))
+            nc.sync.dma_start(out=tile[:].rearrange("p e j c -> p e (j c)"), in_=w1_rows[:, a:b])
+            w1_raw.extend(tile[:, k] for k in range(b - a))
         w2_passes = w2.rearrange("e (q p j) n -> p (e q) (j n)", p=P, j=4)
         w2_raw = {}
-        for a, b in W2_LOADS:
-            w2_raw[a] = raw.tile([P, b - a, 4, N], F32, name="raw", align_bytes=256)
+        for k, (a, b) in enumerate(W2_LOADS):
+            size = 2 if k < 2 else 1
+            w2_raw[a] = raw.tile([P, b - a, 4, N], F32, name="raw_%d" % size, align_bytes=256, bufs=4 // size)
             nc.sync.dma_start(out=w2_raw[a][:].rearrange("p q j n -> p q (j n)"), in_=w2_passes[:, a:b])
         last_raw = []
         for q in range(2):

@@ -112,8 +112,8 @@ def tile_routed_moe_kernel(tc, xT, w1, w2, gate, offs, pos1, pos2, out):
 
         def quant_w2(grouped, n, words=None):
             if words is None:
-                words = work.tile([P, n * N], U32, name="w2_words", align_bytes=64, bufs=8)
-            scales = work.tile([P, n * N], U8, name="w2_scales", align_bytes=64, bufs=8)
+                words = work.tile([P, n * N], U32, name="w2_words", align_bytes=64, bufs=12)
+            scales = work.tile([P, n * N], U8, name="w2_scales", align_bytes=64, bufs=12)
             nc.vector.quantize_mx(out=words[:].bitcast(FP8X4), scales=scales[:], in_=grouped)
             return words, scales
 
@@ -189,6 +189,7 @@ def tile_routed_moe_kernel(tc, xT, w1, w2, gate, offs, pos1, pos2, out):
             for e in range(a, b):
                 y_bank[e] = (bank, a, b)
         joint = [w2_raw[0][:, 2 + q].rearrange("p j n -> p (j n)").bitcast(BF16) for q in range(2)]
+        held = []
         for a, b in W2_LOADS[:3]:
             own = [cast_w2(w2_raw[a], k, k + 1, True, joint[k][:, HALF:] if a == 4 else None) for k in range(2)]
             other = cast_w2(w2_raw[a], 2, 4, False)
@@ -198,15 +199,18 @@ def tile_routed_moe_kernel(tc, xT, w1, w2, gate, offs, pos1, pos2, out):
             if a == 4:
                 codes = [quant_w2(joint[k], 2) for k in range(2)]
                 h_codes.append([(codes[q][0], codes[q][1], 0) for q in range(2)])
-                for k in range(2):
-                    layer2(a + k, codes[k], N)
+                held.extend((a + k, codes[k], N) for k in range(2))
             else:
                 codes = [quant_w2(own[k], 1) for k in range(2)]
-                for k in range(2):
-                    layer2(a + k, codes[k], 0)
+                held.extend((a + k, codes[k], 0) for k in range(2))
             codes = quant_w2(other, 2)
-            for k in range(2):
-                layer2(a + 2 + k, codes, k * N)
+            held.extend((a + 2 + k, codes, k * N) for k in range(2))
+            if a == 4:
+                held = held[-2:] + held[:-2]
+            if a >= 4:
+                for args in held:
+                    layer2(*args)
+                held = []
         own = [cast_w2(w2_raw[12], k, k + 1, True) for k in range(2)]
         codes = [quant_w2(own[k], 1) for k in range(2)]
         for k in range(2):

@@ -49,11 +49,9 @@ def tile_routed_moe_kernel(tc, xT, w1, w2, gate, offs, pos1, pos2, out):
             size = 2 if k < 2 else 1
             w2_raw[a] = raw.tile([P, b - a, 4, N], F32, name="raw_%d" % size, align_bytes=256, bufs=4 // size)
             nc.sync.dma_start(out=w2_raw[a][:].rearrange("p q j n -> p q (j n)"), in_=w2_passes[:, a:b])
-        last_raw = []
+        last_raw = keep.tile([P, 2, 4, N], F32, name="turn", align_bytes=256)
         for q in range(2):
-            tile = keep.tile([P, 1, 4, N], F32, name="turn_%d" % q, align_bytes=256)
-            nc.sync.dma_start(out=tile[:].rearrange("p q j n -> p q (j n)"), in_=w2_passes[:, 2 * E - 2 + q:2 * E - 1 + q])
-            last_raw.append(tile)
+            nc.sync.dma_start(out=last_raw[:, q:q + 1].rearrange("p q j n -> p q (j n)"), in_=w2_passes[:, 2 * E - 2 + q:2 * E - 1 + q])
         gate_t = []
         for r, (pos_t, pos) in enumerate(((pos1_t, pos1), (pos2_t, pos2))):
             tile = keep.tile([P, T], F32, name="gate_%d" % r, align_bytes=256)
@@ -211,19 +209,26 @@ def tile_routed_moe_kernel(tc, xT, w1, w2, gate, offs, pos1, pos2, out):
                 for args in held:
                     layer2(*args)
                 held = []
-        own = [cast_w2(w2_raw[12], k, k + 1, True) for k in range(2)]
+        shared = work.tile([P, HALF], BF16, name="w2_bf", align_bytes=64, bufs=6)
+        src = w2_raw[12][:, 1].rearrange("p j (c i) -> p c j i", i=4)
+        dst = shared[:].rearrange("p (c i j) -> p c j i", i=4, j=4)
+        own = [cast_w2(w2_raw[12], 0, 1, True), shared[:]]
+        nc.scalar.copy(out=dst[:, :20], in_=src[:, :20])
+        nc.vector.tensor_copy(out=dst[:, 20:], in_=src[:, 20:])
         codes = [quant_w2(own[k], 1) for k in range(2)]
         for k in range(2):
             layer2(12 + k, codes[k], 0)
-        layer2(2 * E - 2, quant_w2(cast_w2(last_raw[0], 0, 1, False), 1), 0)
-        final = work.tile([P, HALF], BF16, name="w2_bf", align_bytes=64, bufs=6)
-        src = last_raw[1][:, 0].rearrange("p j (c i) -> p c j i", i=4)
-        dst = final[:].rearrange("p (c i j) -> p c j i", i=4, j=4)
-        nc.scalar.copy(out=dst[:, :16], in_=src[:, :16])
-        nc.vector.tensor_copy(out=dst[:, 16:], in_=src[:, 16:])
-        layer2(2 * E - 1, quant_w2(final[:], 1), 0)
+        final = keep.tile([P, 2 * HALF], BF16, name="final", align_bytes=64)
+        src = last_raw[:].rearrange("p q j (c i) -> p q c j i", i=4)
+        dst = final[:].rearrange("p (q c i j) -> p q c j i", q=2, i=4, j=4)
+        nc.scalar.copy(out=dst[:, 0, 2:], in_=src[:, 0, 2:])
+        nc.scalar.copy(out=dst[:, :, :2], in_=src[:, :, :2])
+        nc.scalar.copy(out=dst[:, 1, 2:10], in_=src[:, 1, 2:10])
+        nc.vector.tensor_copy(out=dst[:, 1, 10:], in_=src[:, 1, 10:])
+        for q in range(2):
+            layer2(2 * E - 2 + q, quant_w2(final[:, q * HALF:(q + 1) * HALF], 1), 0)
 
-        y_all = keep.tile([P, S], F32, name="turn_1", align_bytes=256)
+        y_all = keep.tile([P, S], F32, name="turn", align_bytes=256)
         for k, (lo, hi) in enumerate(Y_BANKS):
             if k == 1:
                 nc.vector.tensor_copy(out=y_all[:, lo * C:hi * C], in_=y_bank[lo][0][:])

@@ -9,16 +9,17 @@ U16 = mybir.dt.uint16
 U8 = mybir.dt.uint8
 FP8X4 = mybir.dt.float8_e4m3fn_x4
 RELU = mybir.ActivationFunctionType.Relu
+COPY = mybir.ActivationFunctionType.Copy
 MULT = mybir.AluOpType.mult
 
 P = 128
 K, T, E, C, H, N = 512, 512, 8, 128, 1024, 128
 S = E * C
-HALF = 512
-W2_LOADS = ((0, 4), (4, 8), (8, 12), (12, 14))
-Y_BANKS = ((0, 4), (4, 7), (7, 8))
+PASS = 512
 W1_LOADS = ((0, 2), (2, 4), (4, 5), (5, 6), (6, 7), (7, 8))
-SHARED = (3, 4, 6)
+W2_LOADS = ((0, 4), (4, 8), (8, 12), (12, 14), (14, 15), (15, 16))
+SCALAR_ROWS = 64
+Y_BANKS = ((0, 4), (4, 7), (7, 8))
 FLOPS = 2 * S * K * H + 2 * S * H * N
 
 
@@ -26,14 +27,13 @@ def tile_routed_moe_kernel(tc, xT, w1, w2, gate, offs, pos1, pos2, out):
     nc = tc.nc
     with ExitStack() as ctx:
         keep = ctx.enter_context(tc.tile_pool(name="keep", bufs=1))
-        raw = ctx.enter_context(tc.tile_pool(name="raw", bufs=8))
+        raw = ctx.enter_context(tc.tile_pool(name="raw", bufs=1))
         work = ctx.enter_context(tc.tile_pool(name="work", bufs=3))
-        ps_a = ctx.enter_context(tc.psum_pool(name="ps_a", bufs=5))
+        ps_h = ctx.enter_context(tc.psum_pool(name="ps_h", bufs=5))
         ps_y = ctx.enter_context(tc.psum_pool(name="ps_y", bufs=3))
 
         offs_t = keep.tile([P, S // 16], U16, align_bytes=128)
-        pos1_t = keep.tile([P, T // 16], U16, align_bytes=64)
-        pos2_t = keep.tile([P, T // 16], U16, align_bytes=64)
+        pos_t = [keep.tile([P, T // 16], U16, name="pos_%d" % r, align_bytes=64) for r in range(2)]
         x_raw = keep.tile([P, 4, T], F32, align_bytes=256)
         nc.sync.dma_start(out=x_raw[:], in_=xT.rearrange("(p j) t -> p j t", j=4))
         nc.sync.dma_start(offs_t[:], offs)
@@ -44,20 +44,35 @@ def tile_routed_moe_kernel(tc, xT, w1, w2, gate, offs, pos1, pos2, out):
             nc.sync.dma_start(out=tile[:].rearrange("p e j c -> p e (j c)"), in_=w1_rows[:, a:b])
             w1_raw.extend(tile[:, k] for k in range(b - a))
         w2_passes = w2.rearrange("e (q p j) n -> p (e q) (j n)", p=P, j=4)
-        w2_raw = {}
+        w2_raw = []
+        w2_load = {}
         for k, (a, b) in enumerate(W2_LOADS):
-            size = 2 if k < 2 else 1
-            w2_raw[a] = raw.tile([P, b - a, 4, N], F32, name="raw_%d" % size, align_bytes=256, bufs=4 // size)
-            nc.sync.dma_start(out=w2_raw[a][:].rearrange("p q j n -> p q (j n)"), in_=w2_passes[:, a:b])
-        last_raw = keep.tile([P, 2, 4, N], F32, name="turn", align_bytes=256)
-        for q in range(2):
-            nc.sync.dma_start(out=last_raw[:, q:q + 1].rearrange("p q j n -> p q (j n)"), in_=w2_passes[:, 2 * E - 2 + q:2 * E - 1 + q])
-        gate_t = []
-        for r, (pos_t, pos) in enumerate(((pos1_t, pos1), (pos2_t, pos2))):
-            tile = keep.tile([P, T], F32, name="gate_%d" % r, align_bytes=256)
-            nc.sync.dma_start(out=tile[:], in_=gate[r])
-            nc.sync.dma_start(pos_t[:], pos)
-            gate_t.append(tile)
+            if k == len(W2_LOADS) - 1:
+                tile = keep.tile([P, 1, 4, N], F32, name="turn", align_bytes=256)
+            else:
+                size = 2 if k < 2 else 1
+                tile = raw.tile([P, b - a, 4, N], F32, name="raw_%d" % size, align_bytes=256, bufs=4 // size)
+            nc.sync.dma_start(out=tile[:].rearrange("p q j n -> p q (j n)"), in_=w2_passes[:, a:b])
+            w2_load[a] = tile
+            w2_raw.extend(tile[:, g] for g in range(b - a))
+        nc.sync.dma_start(pos_t[0][:], pos1)
+        nc.sync.dma_start(pos_t[1][:], pos2)
+        gate_t = [keep.tile([P, T], F32, name="gate_%d" % r, align_bytes=256) for r in range(2)]
+        for r in (1, 0):
+            nc.sync.dma_start(out=gate_t[r][:], in_=gate[r])
+
+        def copy_on(on_vector, dst, src):
+            if on_vector:
+                nc.vector.tensor_copy(out=dst, in_=src)
+            else:
+                nc.scalar.copy(out=dst, in_=src)
+
+        def quantise(values, name, bufs):
+            width = values.shape[1] // 4
+            words = work.tile([P, width], U32, name=name + "_words", align_bytes=64, bufs=bufs)
+            scales = work.tile([P, width], U8, name=name + "_scales", align_bytes=64, bufs=bufs)
+            nc.vector.quantize_mx(out=words[:].bitcast(FP8X4), scales=scales[:], in_=values)
+            return [(words[:, c:c + P].bitcast(FP8X4), scales[:, c:c + P]) for c in range(0, width, P)]
 
         x_bf = keep.tile([P, T, 4], BF16, align_bytes=64)
         x_words = keep.tile([P, T], U32, align_bytes=64)
@@ -65,184 +80,129 @@ def tile_routed_moe_kernel(tc, xT, w1, w2, gate, offs, pos1, pos2, out):
         nc.gpsimd.memset(x_bytes[:], 0)
         x_src = x_raw[:].rearrange("p j (c i) -> p c j i", i=4)
         x_dst = x_bf[:].rearrange("p (c i) j -> p c j i", i=4)
-        nc.vector.tensor_copy(out=x_dst[:, 0:64], in_=x_src[:, 0:64])
-        nc.scalar.copy(out=x_dst[:, 64:128], in_=x_src[:, 64:128])
+        copy_on(True, x_dst[:, :64], x_src[:, :64])
+        copy_on(False, x_dst[:, 64:], x_src[:, 64:])
         nc.vector.quantize_mx(out=x_words[:].bitcast(FP8X4), scales=x_bytes[:], in_=x_bf[:].rearrange("p t j -> p (t j)"))
         g_words = keep.tile([P, S], U32, align_bytes=64)
         g_bytes = keep.tile([P, S], U8, align_bytes=64)
+        for a, b in ((0, 256), (256, 640), (640, S)):
+            entries = offs_t[:, a // 16:b // 16]
+            nc.vector.tensor_copy(g_words[:, a:b], x_words[:].indirect(entries))
+            nc.vector.tensor_copy(g_bytes[:, a:b], x_bytes[:].indirect(entries))
 
-        def gather(a, b):
-            lst = offs_t[:, a // 16:b // 16]
-            nc.vector.tensor_copy(g_words[:, a:b], x_words[:].indirect(lst))
-            nc.vector.tensor_copy(g_bytes[:, a:b], x_bytes[:].indirect(lst))
+        def cast_w1(e, q, u, dst, on_vector, rows=slice(0, P)):
+            src = w1_raw[e][:, :, q * PASS:(q + 1) * PASS].rearrange("p j (m u v) -> p u m j v", u=2, v=2)
+            copy_on(on_vector, dst.rearrange("p (v m j) -> p m j v", v=2, j=4)[:, rows], src[:, u, rows])
 
-        gathers = {0: (0, 256), 1: (256, 640), 2: (640, 1024)}
-
-        def cast_w1(e, q, grouped, on_vector, u=None):
-            src = w1_raw[e][:, :, q * HALF:(q + 1) * HALF].rearrange("p j (m u v) -> p u m j v", u=2, v=2)
-            if u is None:
-                dst = grouped.rearrange("p (u v m j) -> p u m j v", u=2, v=2, j=4)
-            else:
-                src = src[:, u]
-                dst = grouped.rearrange("p (v m j) -> p m j v", v=2, j=4)
-            if on_vector:
-                nc.vector.tensor_copy(out=dst, in_=src)
-            else:
-                nc.scalar.copy(out=dst, in_=src)
-
-        def quant_w1(grouped, n):
-            words = work.tile([P, n * P], U32, name="w1_words", align_bytes=64, bufs=5)
-            scales = work.tile([P, n * P], U8, name="w1_scales", align_bytes=64, bufs=5)
-            nc.vector.quantize_mx(out=words[:].bitcast(FP8X4), scales=scales[:], in_=grouped)
-            return [(words, scales, k * P) for k in range(n)]
-
-        def cast_w2(tile, a, b, on_vector, grouped=None):
-            if grouped is None:
-                fresh = work.tile([P, (b - a) * HALF], BF16, name="w2_bf", align_bytes=64, bufs=6)
-                grouped = fresh[:]
-            src = tile[:, a:b].rearrange("p q j (c i) -> p q c j i", i=4)
-            dst = grouped.rearrange("p (q c i j) -> p q c j i", q=b - a, i=4, j=4)
-            if on_vector:
-                nc.vector.tensor_copy(out=dst, in_=src)
-            else:
-                nc.scalar.copy(out=dst, in_=src)
-            return grouped
-
-        def quant_w2(grouped, n, words=None):
-            if words is None:
-                words = work.tile([P, n * N], U32, name="w2_words", align_bytes=64, bufs=12)
-            scales = work.tile([P, n * N], U8, name="w2_scales", align_bytes=64, bufs=12)
-            nc.vector.quantize_mx(out=words[:].bitcast(FP8X4), scales=scales[:], in_=grouped)
-            return words, scales
+        def cast_upper(e, dst):
+            src = w1_raw[e][:, :, PASS:].rearrange("p j (m u v) -> p u m j v", u=2, v=2)
+            nc.vector.tensor_copy(out=dst.rearrange("p (u v m j) -> p u m j v", u=2, v=2, j=4), in_=src)
 
         def layer1(e, blocks):
-            bank = ps_a.tile([P, 4 * C], F32, name="h_bank")
+            bank = ps_h.tile([P, 4 * C], F32, name="h_bank")
             slots = slice(e * C, (e + 1) * C)
-            for t, (words, scales, col) in enumerate(blocks):
+            for t, (words, scales) in enumerate(blocks):
                 nc.tensor.matmul_mx(
-                    out=bank[:, t * C:(t + 1) * C],
-                    lhsT=words[:, col:col + P].bitcast(FP8X4), lhsT_scale=scales[:, col:col + P],
-                    rhs=g_words[:, slots].bitcast(FP8X4), rhs_scale=g_bytes[:, slots],
-                    start=True, stop=True,
+                    out=bank[:, t * C:(t + 1) * C], lhsT=words, lhsT_scale=scales,
+                    rhs=g_words[:, slots].bitcast(FP8X4), rhs_scale=g_bytes[:, slots], start=True, stop=True,
                 )
             return bank
 
         def relu(bank, h):
-            src = bank[:].rearrange("p (t n) -> p n t", t=4)
-            nc.scalar.activation(out=h.rearrange("p (n t) -> p n t", t=4), in_=src, func=RELU)
-
-        def hidden(banks, h):
-            for q in (1, 0):
-                relu(banks[q], h[:, q * HALF:(q + 1) * HALF])
-            words = work.tile([P, 2 * C], U32, name="h_words", align_bytes=64, bufs=E)
-            scales = work.tile([P, 2 * C], U8, name="h_scales", align_bytes=64, bufs=E)
-            nc.vector.quantize_mx(out=words[:].bitcast(FP8X4), scales=scales[:], in_=h)
-            return [(words, scales, q * C) for q in range(2)]
-
-        def layer2(g, w, col):
-            e, q = divmod(g, 2)
-            bank, lo, hi = y_bank[e]
-            h_words, h_scales, h_col = h_codes[e][q]
-            nc.tensor.matmul_mx(
-                out=bank[:, (e - lo) * C:(e - lo + 1) * C],
-                lhsT=w[0][:, col:col + N].bitcast(FP8X4), lhsT_scale=w[1][:, col:col + N],
-                rhs=h_words[:, h_col:h_col + C].bitcast(FP8X4), rhs_scale=h_scales[:, h_col:h_col + C],
-                start=(q == 0), stop=(q == 1),
-            )
+            nc.scalar.activation(out=h.rearrange("p (n t) -> p n t", t=4), in_=bank[:].rearrange("p (t n) -> p n t", t=4), func=RELU)
 
         h_codes = []
-        banks = {}
-        for e in range(E - 1):
-            if e in gathers:
-                gather(*gathers[e])
-            upper = work.tile([P, 4 * HALF], BF16, name="w1_bf", align_bytes=64, bufs=4)
-            lower = work.tile([P, 4 * HALF], BF16, name="w1_bf", align_bytes=64, bufs=4)
-            cast_w1(e, 1, upper[:], True)
-            if e in SHARED:
-                cast_w1(e, 0, lower[:, :H], False, 0)
-                cast_w1(e, 0, lower[:, H:], True, 1)
+        joint = work.tile([P, 2 * H], BF16, name="joint", align_bytes=64, bufs=2)
+        last_h = [w2_raw[2 + q].rearrange("p j n -> p (j n)").bitcast(BF16) for q in range(2)]
+        for e in range(E):
+            upper = work.tile([P, 2 * H], BF16, name="upper", align_bytes=64, bufs=2)
+            second = work.tile([P, H], BF16, name="second", align_bytes=64, bufs=2)
+            cast_upper(e, upper[:])
+            cast_w1(e, 0, 0, joint[:, H:], False)
+            cast_w1(e, 0, 1, second[:], False, slice(0, SCALAR_ROWS))
+            cast_w1(e, 0, 1, second[:], True, slice(SCALAR_ROWS, P))
+            banks = {1: layer1(e, quantise(upper[:], "upper", 2))}
+            if e == 0:
+                first = quantise(joint[:, H:], "joint", E)
             else:
-                cast_w1(e, 0, lower[:], False)
-            prev = banks
-            banks = {1: layer1(e, quant_w1(upper[:], 4)), 0: layer1(e, quant_w1(lower[:], 4))}
-            if e > 0:
-                h_codes.append(hidden(prev, w1_raw[e][:, 3, HALF:H].bitcast(BF16)))
-        first = keep.tile([P, 2 * H], BF16, name="first", align_bytes=64)
-        second = work.tile([P, H], BF16, name="w1_bf", align_bytes=64, bufs=4)
-        lower = work.tile([P, 4 * HALF], BF16, name="w1_bf", align_bytes=64, bufs=4)
-        for q in (1, 0):
-            relu(banks[q], first[:, q * HALF:(q + 1) * HALF])
-        cast_w1(E - 1, 1, first[:, H:], True, 0)
-        cast_w1(E - 1, 1, second[:], True, 1)
-        cast_w1(E - 1, 0, lower[:], False)
-        words = keep.tile([P, HALF], U32, name="first_words", align_bytes=64)
-        scales = keep.tile([P, HALF], U8, name="first_scales", align_bytes=64)
-        nc.vector.quantize_mx(out=words[:].bitcast(FP8X4), scales=scales[:], in_=first[:])
-        blocks = [(words, scales, k * P) for k in range(4)]
-        h_codes.append(blocks[:2])
-        banks = {1: layer1(E - 1, blocks[2:] + quant_w1(second[:], 2)), 0: layer1(E - 1, quant_w1(lower[:], 4))}
+                blocks = quantise(joint[:], "joint", E)
+                h_codes.append(blocks[:2])
+                first = blocks[2:]
+            banks[0] = layer1(e, first + quantise(second[:], "second", 2))
+            if e < E - 1:
+                joint = work.tile([P, 2 * H], BF16, name="joint", align_bytes=64, bufs=2)
+                for q in (1, 0):
+                    relu(banks[q], joint[:, q * PASS:(q + 1) * PASS])
+
+        def cast_w2(g, dst, on_vector, groups=slice(0, N // 4)):
+            src = w2_raw[g].rearrange("p j (c i) -> p c j i", i=4)
+            copy_on(on_vector, dst.rearrange("p (c i j) -> p c j i", i=4, j=4)[:, groups], src[:, groups])
+
         y_bank = {}
         for a, b in Y_BANKS:
             bank = ps_y.tile([P, (b - a) * C], F32, name="y_bank")
             for e in range(a, b):
-                y_bank[e] = (bank, a, b)
-        joint = [w2_raw[0][:, 2 + q].rearrange("p j n -> p (j n)").bitcast(BF16) for q in range(2)]
-        held = []
-        for a, b in W2_LOADS[:3]:
-            own = [cast_w2(w2_raw[a], k, k + 1, True, joint[k][:, HALF:] if a == 4 else None) for k in range(2)]
-            other = cast_w2(w2_raw[a], 2, 4, False)
+                y_bank[e] = bank[:, (e - a) * C:(e - a + 1) * C]
+            y_bank[a, b] = bank
+
+        def layer2(g, block):
+            e, q = divmod(g, 2)
+            nc.tensor.matmul_mx(
+                out=y_bank[e], lhsT=block[0], lhsT_scale=block[1], rhs=h_codes[e][q][0], rhs_scale=h_codes[e][q][1],
+                start=(q == 0), stop=(q == 1),
+            )
+
+        w2_codes = {}
+        for a in (0, 4, 8):
+            staged = []
+            for k in range(2):
+                if a == 4:
+                    dst = last_h[k][:, PASS:]
+                    staged.append(last_h[k])
+                else:
+                    single = work.tile([P, PASS], BF16, name="w2_bf", align_bytes=64, bufs=6)
+                    dst = single[:]
+                    staged.append(dst)
+                cast_w2(a + k, dst, True)
+            pair = work.tile([P, 2 * PASS], BF16, name="w2_bf", align_bytes=64, bufs=6)
+            src = w2_load[a][:, 2:4].rearrange("p q j (c i) -> p q c j i", i=4)
+            nc.scalar.copy(out=pair[:].rearrange("p (q c i j) -> p q c j i", q=2, i=4, j=4), in_=src)
             if a == 0:
                 for q in (1, 0):
-                    relu(banks[q], joint[q][:, :HALF])
+                    relu(banks[q], last_h[q][:, :PASS])
+            blocks = [quantise(values, "w2", 12) for values in staged]
             if a == 4:
-                codes = [quant_w2(joint[k], 2) for k in range(2)]
-                h_codes.append([(codes[q][0], codes[q][1], 0) for q in range(2)])
-                held.extend((a + k, codes[k], N) for k in range(2))
-            else:
-                codes = [quant_w2(own[k], 1) for k in range(2)]
-                held.extend((a + k, codes[k], 0) for k in range(2))
-            codes = quant_w2(other, 2)
-            held.extend((a + 2 + k, codes, k * N) for k in range(2))
-            if a == 4:
-                held = held[-2:] + held[:-2]
-            if a >= 4:
-                for args in held:
-                    layer2(*args)
-                held = []
-        shared = work.tile([P, HALF], BF16, name="w2_bf", align_bytes=64, bufs=6)
-        src = w2_raw[12][:, 1].rearrange("p j (c i) -> p c j i", i=4)
-        dst = shared[:].rearrange("p (c i j) -> p c j i", i=4, j=4)
-        own = [cast_w2(w2_raw[12], 0, 1, True), shared[:]]
-        nc.scalar.copy(out=dst[:, :20], in_=src[:, :20])
-        nc.vector.tensor_copy(out=dst[:, 20:], in_=src[:, 20:])
-        codes = [quant_w2(own[k], 1) for k in range(2)]
-        for k in range(2):
-            layer2(12 + k, codes[k], 0)
-        final = keep.tile([P, 2 * HALF], BF16, name="final", align_bytes=64)
-        src = last_raw[:].rearrange("p q j (c i) -> p q c j i", i=4)
-        dst = final[:].rearrange("p (q c i j) -> p q c j i", q=2, i=4, j=4)
-        nc.scalar.copy(out=dst[:, 0, 2:], in_=src[:, 0, 2:])
-        nc.scalar.copy(out=dst[:, :, :2], in_=src[:, :, :2])
-        nc.scalar.copy(out=dst[:, 1, 2:10], in_=src[:, 1, 2:10])
-        nc.vector.tensor_copy(out=dst[:, 1, 10:], in_=src[:, 1, 10:])
-        for q in range(2):
-            layer2(2 * E - 2 + q, quant_w2(final[:, q * HALF:(q + 1) * HALF], 1), 0)
+                h_codes.append([blocks[q][0] for q in range(2)])
+            for k in range(2):
+                w2_codes[a + k] = blocks[k][-1]
+            w2_codes[a + 2], w2_codes[a + 3] = quantise(pair[:], "w2", 12)
+        for g in (6, 7, 0, 1, 2, 3, 4, 5, 8, 9, 10, 11):
+            layer2(g, w2_codes[g])
+        for g, on_scalar in ((12, 0), (13, 20), (14, 32), (15, 12)):
+            single = work.tile([P, PASS], BF16, name="w2_bf", align_bytes=64, bufs=6)
+            if on_scalar > 0:
+                cast_w2(g, single[:], False, slice(0, on_scalar))
+            if on_scalar < N // 4:
+                cast_w2(g, single[:], True, slice(on_scalar, N // 4))
+            w2_codes[g] = single
+            if g % 2 == 1:
+                for done in (g - 1, g):
+                    layer2(done, quantise(w2_codes[done][:], "w2", 12)[0])
 
         y_all = keep.tile([P, S], F32, name="turn", align_bytes=256)
-        for k, (lo, hi) in enumerate(Y_BANKS):
-            if k == 1:
-                nc.vector.tensor_copy(out=y_all[:, lo * C:hi * C], in_=y_bank[lo][0][:])
-            else:
-                nc.scalar.copy(out=y_all[:, lo * C:hi * C], in_=y_bank[lo][0][:])
+        for k, (a, b) in enumerate(Y_BANKS):
+            copy_on(k == 1, y_all[:, a * C:b * C], y_bank[a, b][:])
 
-        part1 = keep.tile([P, T], F32)
-        nc.vector.tensor_tensor(part1[:], y_all[:].indirect(pos1_t[:]), gate_t[0][:], MULT)
-        pieces = ((0, 256), (256, T))
-        part2 = {}
-        for a, b in pieces:
-            part2[a] = keep.tile([P, b - a], F32, name="part2_%d" % a)
-            nc.vector.tensor_tensor(part2[a][:], y_all[:].indirect(pos2_t[:, a // 16:b // 16]), gate_t[1][:, a:b], MULT)
-        for a, b in pieces:
-            result = keep.tile([P, b - a], F32, name="result_%d" % a, align_bytes=256)
-            nc.vector.tensor_add(result[:], part1[:, a:b], part2[a][:])
+        halves = ((0, T // 2), (T // 2, T))
+        second_part = keep.tile([P, T], F32, name="x_bf", align_bytes=64)
+        nc.vector.tensor_tensor(second_part[:], y_all[:].indirect(pos_t[1][:]), gate_t[1][:], MULT)
+        first_part = {}
+        for a, b in halves:
+            picked = keep.tile([P, b - a], F32, name="g_words" if a else "x_words", align_bytes=64)
+            nc.scalar.activation(picked[:], y_all[:].indirect(pos_t[0][:, a // 16:b // 16]), COPY)
+            first_part[a] = keep.tile([P, b - a], F32, name="first_part_%d" % a)
+            nc.vector.tensor_tensor(first_part[a][:], picked[:], gate_t[0][:, a:b], MULT)
+        for a, b in halves:
+            result = keep.tile([P, b - a], F32, name="result" if a else "x_raw", align_bytes=256)
+            nc.vector.tensor_add(result[:], first_part[a][:], second_part[:, a:b])
             nc.sync.dma_start(out=out[:, a:b], in_=result[:])

@@ -19,6 +19,7 @@ PASS = 512
 W1_LOADS = ((0, 2), (2, 4), (4, 5), (5, 6), (6, 7), (7, 8))
 W2_LOADS = ((0, 4), (4, 8), (8, 12), (12, 14), (14, 15), (15, 16))
 SCALAR_ROWS = 64
+FIRST_GATHER = 288
 Y_BANKS = ((0, 4), (4, 7), (7, 8))
 FLOPS = 2 * S * K * H + 2 * S * H * N
 
@@ -196,13 +197,12 @@ def tile_routed_moe_kernel(tc, xT, w1, w2, gate, offs, pos1, pos2, out):
         halves = ((0, T // 2), (T // 2, T))
         second_part = keep.tile([P, T], F32, name="x_bf", align_bytes=64)
         nc.vector.tensor_tensor(second_part[:], y_all[:].indirect(pos_t[1][:]), gate_t[1][:], MULT)
-        first_part = {}
-        for a, b in halves:
+        first_part = keep.tile([P, T], F32)
+        for a, b in ((0, FIRST_GATHER), (FIRST_GATHER, T)):
             picked = keep.tile([P, b - a], F32, name="g_words" if a else "x_words", align_bytes=64)
             nc.scalar.activation(picked[:], y_all[:].indirect(pos_t[0][:, a // 16:b // 16]), COPY)
-            first_part[a] = keep.tile([P, b - a], F32, name="first_part_%d" % a)
-            nc.vector.tensor_tensor(first_part[a][:], picked[:], gate_t[0][:, a:b], MULT)
+            nc.vector.tensor_tensor(first_part[:, a:b], picked[:], gate_t[0][:, a:b], MULT)
         for a, b in halves:
             result = keep.tile([P, b - a], F32, name="result" if a else "x_raw", align_bytes=256)
-            nc.vector.tensor_add(result[:], first_part[a][:], second_part[:, a:b])
+            nc.vector.tensor_add(result[:], first_part[:, a:b], second_part[:, a:b])
             nc.sync.dma_start(out=out[:, a:b], in_=result[:])

@@ -19,7 +19,7 @@ PASS = 512
 W1_LOADS = ((0, 2), (2, 4), (4, 5), (5, 6), (6, 7), (7, 8))
 W2_LOADS = ((0, 4), (4, 8), (8, 12), (12, 14), (14, 15), (15, 16))
 SCALAR_ROWS = 64
-FIRST_GATHER = 288
+FIRST_GATHER = 320
 Y_BANKS = ((0, 4), (4, 7), (7, 8))
 FLOPS = 2 * S * K * H + 2 * S * H * N
 

from contextlib import ExitStack

import concourse.mybir as mybir

F32 = mybir.dt.float32
BF16 = mybir.dt.bfloat16
U32 = mybir.dt.uint32
U16 = mybir.dt.uint16
U8 = mybir.dt.uint8
FP8X4 = mybir.dt.float8_e4m3fn_x4
RELU = mybir.ActivationFunctionType.Relu
COPY = mybir.ActivationFunctionType.Copy
MULT = mybir.AluOpType.mult

P = 128
K, T, E, C, H, N = 512, 512, 8, 128, 1024, 128
S = E * C
PASS = 512
W1_LOADS = ((0, 2), (2, 4), (4, 5), (5, 6), (6, 7), (7, 8))
W2_LOADS = ((0, 4), (4, 8), (8, 12), (12, 14), (14, 15), (15, 16))
SCALAR_ROWS = 64
FIRST_GATHER = 320
Y_BANKS = ((0, 4), (4, 7), (7, 8))
FLOPS = 2 * S * K * H + 2 * S * H * N


def tile_routed_moe_kernel(tc, xT, w1, w2, gate, offs, pos1, pos2, out):
    nc = tc.nc
    with ExitStack() as ctx:
        keep = ctx.enter_context(tc.tile_pool(name="keep", bufs=1))
        raw = ctx.enter_context(tc.tile_pool(name="raw", bufs=1))
        work = ctx.enter_context(tc.tile_pool(name="work", bufs=3))
        ps_h = ctx.enter_context(tc.psum_pool(name="ps_h", bufs=5))
        ps_y = ctx.enter_context(tc.psum_pool(name="ps_y", bufs=3))

        offs_t = keep.tile([P, S // 16], U16, align_bytes=128)
        pos_t = [keep.tile([P, T // 16], U16, name="pos_%d" % r, align_bytes=64) for r in range(2)]
        x_raw = keep.tile([P, 4, T], F32, align_bytes=256)
        nc.sync.dma_start(out=x_raw[:], in_=xT.rearrange("(p j) t -> p j t", j=4))
        nc.sync.dma_start(offs_t[:], offs)
        w1_raw = []
        w1_rows = w1.rearrange("e (p j) c -> p e (j c)", j=4)
        for a, b in W1_LOADS:
            tile = raw.tile([P, b - a, 4, H], F32, name="raw_%d" % (b - a), align_bytes=256, bufs=4 // (b - a))
            nc.sync.dma_start(out=tile[:].rearrange("p e j c -> p e (j c)"), in_=w1_rows[:, a:b])
            w1_raw.extend(tile[:, k] for k in range(b - a))
        w2_passes = w2.rearrange("e (q p j) n -> p (e q) (j n)", p=P, j=4)
        w2_raw = []
        w2_load = {}
        for k, (a, b) in enumerate(W2_LOADS):
            if k == len(W2_LOADS) - 1:
                tile = keep.tile([P, 1, 4, N], F32, name="turn", align_bytes=256)
            else:
                size = 2 if k < 2 else 1
                tile = raw.tile([P, b - a, 4, N], F32, name="raw_%d" % size, align_bytes=256, bufs=4 // size)
            nc.sync.dma_start(out=tile[:].rearrange("p q j n -> p q (j n)"), in_=w2_passes[:, a:b])
            w2_load[a] = tile
            w2_raw.extend(tile[:, g] for g in range(b - a))
        nc.sync.dma_start(pos_t[0][:], pos1)
        nc.sync.dma_start(pos_t[1][:], pos2)
        gate_t = [keep.tile([P, T], F32, name="gate_%d" % r, align_bytes=256) for r in range(2)]
        for r in (1, 0):
            nc.sync.dma_start(out=gate_t[r][:], in_=gate[r])

        def copy_on(on_vector, dst, src):
            if on_vector:
                nc.vector.tensor_copy(out=dst, in_=src)
            else:
                nc.scalar.copy(out=dst, in_=src)

        def quantise(values, name, bufs):
            width = values.shape[1] // 4
            words = work.tile([P, width], U32, name=name + "_words", align_bytes=64, bufs=bufs)
            scales = work.tile([P, width], U8, name=name + "_scales", align_bytes=64, bufs=bufs)
            nc.vector.quantize_mx(out=words[:].bitcast(FP8X4), scales=scales[:], in_=values)
            return [(words[:, c:c + P].bitcast(FP8X4), scales[:, c:c + P]) for c in range(0, width, P)]

        x_bf = keep.tile([P, T, 4], BF16, align_bytes=64)
        x_words = keep.tile([P, T], U32, align_bytes=64)
        x_bytes = keep.tile([P, T], U8, align_bytes=64)
        nc.gpsimd.memset(x_bytes[:], 0)
        x_src = x_raw[:].rearrange("p j (c i) -> p c j i", i=4)
        x_dst = x_bf[:].rearrange("p (c i) j -> p c j i", i=4)
        copy_on(True, x_dst[:, :64], x_src[:, :64])
        copy_on(False, x_dst[:, 64:], x_src[:, 64:])
        nc.vector.quantize_mx(out=x_words[:].bitcast(FP8X4), scales=x_bytes[:], in_=x_bf[:].rearrange("p t j -> p (t j)"))
        g_words = keep.tile([P, S], U32, align_bytes=64)
        g_bytes = keep.tile([P, S], U8, align_bytes=64)
        for a, b in ((0, 256), (256, 640), (640, S)):
            entries = offs_t[:, a // 16:b // 16]
            nc.vector.tensor_copy(g_words[:, a:b], x_words[:].indirect(entries))
            nc.vector.tensor_copy(g_bytes[:, a:b], x_bytes[:].indirect(entries))

        def cast_w1(e, q, u, dst, on_vector, rows=slice(0, P)):
            src = w1_raw[e][:, :, q * PASS:(q + 1) * PASS].rearrange("p j (m u v) -> p u m j v", u=2, v=2)
            copy_on(on_vector, dst.rearrange("p (v m j) -> p m j v", v=2, j=4)[:, rows], src[:, u, rows])

        def cast_upper(e, dst):
            src = w1_raw[e][:, :, PASS:].rearrange("p j (m u v) -> p u m j v", u=2, v=2)
            nc.vector.tensor_copy(out=dst.rearrange("p (u v m j) -> p u m j v", u=2, v=2, j=4), in_=src)

        def layer1(e, blocks):
            bank = ps_h.tile([P, 4 * C], F32, name="h_bank")
            slots = slice(e * C, (e + 1) * C)
            for t, (words, scales) in enumerate(blocks):
                nc.tensor.matmul_mx(
                    out=bank[:, t * C:(t + 1) * C], lhsT=words, lhsT_scale=scales,
                    rhs=g_words[:, slots].bitcast(FP8X4), rhs_scale=g_bytes[:, slots], start=True, stop=True,
                )
            return bank

        def relu(bank, h):
            nc.scalar.activation(out=h.rearrange("p (n t) -> p n t", t=4), in_=bank[:].rearrange("p (t n) -> p n t", t=4), func=RELU)

        h_codes = []
        joint = work.tile([P, 2 * H], BF16, name="joint", align_bytes=64, bufs=2)
        last_h = [w2_raw[2 + q].rearrange("p j n -> p (j n)").bitcast(BF16) for q in range(2)]
        for e in range(E):
            upper = work.tile([P, 2 * H], BF16, name="upper", align_bytes=64, bufs=2)
            second = work.tile([P, H], BF16, name="second", align_bytes=64, bufs=2)
            cast_upper(e, upper[:])
            cast_w1(e, 0, 0, joint[:, H:], False)
            cast_w1(e, 0, 1, second[:], False, slice(0, SCALAR_ROWS))
            cast_w1(e, 0, 1, second[:], True, slice(SCALAR_ROWS, P))
            banks = {1: layer1(e, quantise(upper[:], "upper", 2))}
            if e == 0:
                first = quantise(joint[:, H:], "joint", E)
            else:
                blocks = quantise(joint[:], "joint", E)
                h_codes.append(blocks[:2])
                first = blocks[2:]
            banks[0] = layer1(e, first + quantise(second[:], "second", 2))
            if e < E - 1:
                joint = work.tile([P, 2 * H], BF16, name="joint", align_bytes=64, bufs=2)
                for q in (1, 0):
                    relu(banks[q], joint[:, q * PASS:(q + 1) * PASS])

        def cast_w2(g, dst, on_vector, groups=slice(0, N // 4)):
            src = w2_raw[g].rearrange("p j (c i) -> p c j i", i=4)
            copy_on(on_vector, dst.rearrange("p (c i j) -> p c j i", i=4, j=4)[:, groups], src[:, groups])

        y_bank = {}
        for a, b in Y_BANKS:
            bank = ps_y.tile([P, (b - a) * C], F32, name="y_bank")
            for e in range(a, b):
                y_bank[e] = bank[:, (e - a) * C:(e - a + 1) * C]
            y_bank[a, b] = bank

        def layer2(g, block):
            e, q = divmod(g, 2)
            nc.tensor.matmul_mx(
                out=y_bank[e], lhsT=block[0], lhsT_scale=block[1], rhs=h_codes[e][q][0], rhs_scale=h_codes[e][q][1],
                start=(q == 0), stop=(q == 1),
            )

        w2_codes = {}
        for a in (0, 4, 8):
            staged = []
            for k in range(2):
                if a == 4:
                    dst = last_h[k][:, PASS:]
                    staged.append(last_h[k])
                else:
                    single = work.tile([P, PASS], BF16, name="w2_bf", align_bytes=64, bufs=6)
                    dst = single[:]
                    staged.append(dst)
                cast_w2(a + k, dst, True)
            pair = work.tile([P, 2 * PASS], BF16, name="w2_bf", align_bytes=64, bufs=6)
            src = w2_load[a][:, 2:4].rearrange("p q j (c i) -> p q c j i", i=4)
            nc.scalar.copy(out=pair[:].rearrange("p (q c i j) -> p q c j i", q=2, i=4, j=4), in_=src)
            if a == 0:
                for q in (1, 0):
                    relu(banks[q], last_h[q][:, :PASS])
            blocks = [quantise(values, "w2", 12) for values in staged]
            if a == 4:
                h_codes.append([blocks[q][0] for q in range(2)])
            for k in range(2):
                w2_codes[a + k] = blocks[k][-1]
            w2_codes[a + 2], w2_codes[a + 3] = quantise(pair[:], "w2", 12)
        for g in (6, 7, 0, 1, 2, 3, 4, 5, 8, 9, 10, 11):
            layer2(g, w2_codes[g])
        for g, on_scalar in ((12, 0), (13, 20), (14, 32), (15, 12)):
            single = work.tile([P, PASS], BF16, name="w2_bf", align_bytes=64, bufs=6)
            if on_scalar > 0:
                cast_w2(g, single[:], False, slice(0, on_scalar))
            if on_scalar < N // 4:
                cast_w2(g, single[:], True, slice(on_scalar, N // 4))
            w2_codes[g] = single
            if g % 2 == 1:
                for done in (g - 1, g):
                    layer2(done, quantise(w2_codes[done][:], "w2", 12)[0])

        y_all = keep.tile([P, S], F32, name="turn", align_bytes=256)
        for k, (a, b) in enumerate(Y_BANKS):
            copy_on(k == 1, y_all[:, a * C:b * C], y_bank[a, b][:])

        halves = ((0, T // 2), (T // 2, T))
        second_part = keep.tile([P, T], F32, name="x_bf", align_bytes=64)
        nc.vector.tensor_tensor(second_part[:], y_all[:].indirect(pos_t[1][:]), gate_t[1][:], MULT)
        first_part = keep.tile([P, T], F32)
        for a, b in ((0, FIRST_GATHER), (FIRST_GATHER, T)):
            picked = keep.tile([P, b - a], F32, name="g_words" if a else "x_words", align_bytes=64)
            nc.scalar.activation(picked[:], y_all[:].indirect(pos_t[0][:, a // 16:b // 16]), COPY)
            nc.vector.tensor_tensor(first_part[:, a:b], picked[:], gate_t[0][:, a:b], MULT)
        for a, b in halves:
            result = keep.tile([P, b - a], F32, name="result" if a else "x_raw", align_bytes=256)
            nc.vector.tensor_add(result[:], first_part[:, a:b], second_part[:, a:b])
            nc.sync.dma_start(out=out[:, a:b], in_=result[:])
